import numpy as np
import ml_dtypes


def mxq(x, axis, fmt="e4m3"):
    dtype, down = {"e4m3": (ml_dtypes.float8_e4m3fn, 7), "e5m2": (ml_dtypes.float8_e5m2, 14)}[fmt]
    v = np.moveaxis(np.asarray(x, np.float32).astype(ml_dtypes.bfloat16).astype(np.float64), axis, -1)
    blocks = v.reshape(v.shape[:-1] + (-1, 32))
    amax = np.abs(blocks).max(-1, keepdims=True)
    byte = np.maximum(np.where(amax > 0, np.frexp(amax)[1] - 1 + 127, 0) - down, 1)
    scale = np.exp2(byte - 127.0)
    codes = (blocks / scale).astype(np.float32).astype(dtype).astype(np.float64)
    return np.moveaxis((codes * scale).reshape(v.shape), -1, axis)


WIDE = False


def mx_kscale(k):
    if not WIDE:
        return np.ones(k)
    levels = np.array([10, -10, 5, -5, 0])
    if k % 512:
        return np.exp2(np.random.permutation(np.resize(levels, k // 32))).repeat(32)
    a = np.empty((k // 512, 16))
    for p in range(k // 512):
        a[p, :8] = np.random.permutation(np.resize(levels, 8))
        for g in range(8):
            far = levels[np.abs(levels - a[p, g]) >= 10]
            a[p, g + 8] = far[np.random.randint(len(far))]
    return np.exp2(a.ravel()).repeat(32)


def f64(x):
    return np.asarray(x).astype(np.float64)


def striped(idx):
    return np.tile(idx.reshape(-1, 16).T, (8, 1)).astype(np.uint16)


def unstriped(offs):
    return offs[:16].T.reshape(-1).astype(np.int64)


def pack_weight(w):
    k, n = w.shape
    w = f64(np.asarray(w, np.float32).astype(ml_dtypes.bfloat16)).reshape(k // 32, 32, n)
    amax = np.abs(w).max(1)
    byte = np.clip(np.where(amax > 0, np.frexp(amax)[1] - 1 + 127 - 7, 1), 1, 254)
    scaled = (w * np.exp2(127.0 - byte)[:, None, :]).reshape(k, n).astype(np.float32)
    words = np.ascontiguousarray(scaled.reshape(k // 512, 128, 4, n).transpose(0, 1, 3, 2)).astype(ml_dtypes.float8_e4m3fn).view(np.uint8)
    return words, np.ascontiguousarray(byte.astype(np.uint8).reshape(k // 512, 16, n))


def unpack_weight(words, scales):
    g, p, n, _ = words.shape
    vals = np.ascontiguousarray(words).view(ml_dtypes.float8_e4m3fn).astype(np.float64) * np.repeat(np.exp2(scales.astype(np.float64) - 127.0), 8, axis=1)[..., None]
    return vals.transpose(0, 1, 3, 2).reshape(g * 512, n)


E2M1 = np.array([0.0, 0.5, 1.0, 1.5, 2.0, 3.0, 4.0, 6.0, -0.0, -0.5, -1.0, -1.5, -2.0, -3.0, -4.0, -6.0])


def pack_fp4(w):
    k, n = w.shape
    w = f64(np.asarray(w, np.float32).astype(ml_dtypes.bfloat16)).reshape(k // 32, 32, n)
    amax = np.abs(w).max(1)
    mant, ex = np.frexp(amax / 6.0)
    byte = np.clip(np.where(amax > 0, np.where(mant > 0.5, ex, ex - 1) + 127, 1), 1, 254)
    scaled = (w * np.exp2(127.0 - byte)[:, None, :]).reshape(k, n).astype(np.float32)
    c = np.ascontiguousarray(scaled.reshape(k // 512, 128, 4, n).transpose(0, 1, 3, 2)).astype(ml_dtypes.float4_e2m1fn).view(np.uint8) & 0xF
    words = (c[..., 0::2] | (c[..., 1::2] << 4)).reshape(k // 512, 128, 2 * n)
    return np.ascontiguousarray(words), np.ascontiguousarray(byte.astype(np.uint8).reshape(k // 512, 16, n))


def unpack_fp4(words, scales):
    g, _, n = scales.shape
    words = np.ascontiguousarray(words).reshape(g, 128, n, 2)
    nib = np.empty((g, 128, n, 4), np.uint8)
    nib[..., 0::2] = words & 0xF
    nib[..., 1::2] = words >> 4
    vals = E2M1[nib] * np.repeat(np.exp2(scales.astype(np.float64) - 127.0), 8, axis=1)[..., None]
    return vals.transpose(0, 1, 3, 2).reshape(g * 512, n)


def planes(y):
    n, m = y.shape
    v = y.astype(np.float32).astype(ml_dtypes.bfloat16).astype(np.float64).reshape(n // 32, 32, m)
    top = np.abs(v).max(1)
    byte = np.clip(np.where(top > 0, np.frexp(top)[1] - 1 + 127 - 7, 1), 1, 254)
    codes = (v * np.exp2(127.0 - byte)[:, None, :]).reshape(n, m).astype(np.float32).astype(ml_dtypes.float8_e4m3fn).view(np.uint8)
    words = codes.reshape(n // 512, 128, 4, m).transpose(0, 1, 3, 2)
    return np.ascontiguousarray(words), np.ascontiguousarray(byte.astype(np.uint8).reshape(n // 512, 16, m))


K, T, S, D, V, H, N = 1024, 2048, 1024, 2, 512, 512, 512
P = 2 ** 7


def setup_inputs():
    n = np.random.standard_normal
    s = mx_kscale(K)[:, None]
    u = mx_kscale(H)
    packed_xT = pack_weight(n((K, T)) * s)
    packed_w2 = pack_fp4(n((H, N)) / np.sqrt(H) / u[:, None])
    return {
        "x_words": packed_xT[0],
        "x_scales": packed_xT[1],
        "w1": (n((K, H)) / np.sqrt(K) / s * u).astype(np.float32),
        "w2_words": packed_w2[0],
        "w2_scales": packed_w2[1],
        "gate": (np.tile(np.random.uniform(0.2, 1.0, (D, 1, V)), (1, P, 1))).astype(np.float32),
        "offs": striped(np.random.permutation(T)[:S]),
    }


def reference(x_words, x_scales, w1, w2_words, w2_scales, gate, offs):
    xq = unpack_weight(x_words, x_scales)[:, unstriped(offs)]
    w1q = mxq(f64(w1), 0, "e4m3")
    y0 = w1q.T @ xq[:, :V]
    y1 = w1q.T @ xq[:, V:2 * V]
    z = y0 * f64(gate)[0, :1] + y1 * f64(gate)[1, :1]
    out_0 = unpack_fp4(w2_words, w2_scales).T @ mxq(z, 0, "e4m3")
    return (out_0,) + planes(out_0)

@@ -1,0 +1,203 @@
+from contextlib import ExitStack
+
+import concourse.mybir as mybir
+from concourse.masks import make_identity
+
+K, T, S, D, V, H, N = 1024, 2048, 1024, 2, 512, 512, 512
+FLOPS = 2 * K * H * S + 2 * H * N * V
+
+F32 = mybir.dt.float32
+BF16 = mybir.dt.bfloat16
+I32 = mybir.dt.int32
+U32 = mybir.dt.uint32
+U16 = mybir.dt.uint16
+U8 = mybir.dt.uint8
+FP8X4 = mybir.dt.float8_e4m3fn_x4
+FP4X4 = mybir.dt.float4_e2m1fn_x4
+COPY = mybir.ActivationFunctionType.Copy
+MULT = mybir.AluOpType.mult
+ADD = mybir.AluOpType.add
+
+P = 128
+PACK = 4
+K_PASS = P * PACK
+PASSES = K // K_PASS
+CHUNKS = V // P
+QUADS = 4
+HALF = H // 2
+
+
+def round_and_interleave(engine_copies, grouped, raw):
+    dst = grouped.rearrange("p (u m e j) -> p m j u e", u=2, e=2, j=PACK)
+    src = raw.rearrange("p j (m u e) -> p m j u e", u=2, e=2)
+    share = 2 // len(engine_copies)
+    for n, engine_copy in enumerate(engine_copies):
+        us = slice(n * share, (n + 1) * share)
+        engine_copy(out=dst[:, :, :, us, :], in_=src[:, :, :, us, :])
+
+
+def tile_picked_zbloom_none_po_kernel(
+    tc, x_words, x_scales, w1, w2_words, w2_scales, gate, offs, out_0, out_1, out_2
+):
+    nc = tc.nc
+    with ExitStack() as ctx:
+        keep = ctx.enter_context(tc.tile_pool(name="keep", bufs=1))
+        ring = ctx.enter_context(tc.tile_pool(name="ring", bufs=4))
+        psum = ctx.enter_context(tc.psum_pool(name="psum", bufs=2))
+
+        offsets = keep.tile([P, S // 16], U16, name="offsets")
+        nc.sync.dma_start(offsets[:], offs)
+
+        xs_table = keep.tile([P, T], U8, name="xs_table", align_bytes=64)
+        nc.vector.memset(xs_table[:].bitcast(I32), 0)
+        gate_rows = keep.tile([P, P], F32, name="gate_rows")
+        nc.gpsimd.memset(gate_rows[:], 0.0)
+
+        ident = keep.tile([P, P], F32, name="ident")
+        make_identity(nc, ident[:])
+        w2s_raw = keep.tile([P, N], U8, name="w2s_raw", align_bytes=64)
+        nc.gpsimd.memset(w2s_raw[:].bitcast(I32), 0)
+
+        w2w_raw = keep.tile([P, 2 * N], U8, name="w2w_raw")
+        nc.sync.dma_start(out=w2w_raw[:].bitcast(I32), in_=w2_words[0].bitcast(I32))
+
+        xw_table = [keep.tile([P, T], I32, name="xw_table%d" % g, align_bytes=64) for g in range(PASSES)]
+        w1_rows = [w1[g * K_PASS : (g + 1) * K_PASS, :].rearrange("(p j) c -> p j c", j=PACK) for g in range(PASSES)]
+
+        def load_x(g):
+            nc.sync.dma_start(out=xw_table[g][:], in_=x_words[g].rearrange("p n t -> p (n t)").bitcast(I32))
+
+        def load_w1(g, h, tag):
+            raw = keep.tile([P, PACK, HALF], F32, name="w1_raw%d%d" % (g, h), tag=tag)
+            nc.sync.dma_start(out=raw[:], in_=w1_rows[g][:, :, h * HALF : (h + 1) * HALF])
+            return raw
+
+        nc.sync.dma_start(
+            out=gate_rows[0 : D * CHUNKS, :], in_=gate[:, 0, :].rearrange("d (c p) -> d c p", p=P)
+        )
+        for q, queue in enumerate((nc.sync, nc.scalar, nc.sync, nc.scalar)):
+            queue.dma_start(
+                out=xs_table[32 * q : 32 * q + 4 * PASSES, :].bitcast(I32),
+                in_=x_scales[:, 4 * q : 4 * q + 4, :].bitcast(I32),
+            )
+        load_x(0)
+        raw00 = load_w1(0, 0, "stage0")
+        raw01 = load_w1(0, 1, "stage1")
+        load_x(1)
+
+        gate_ps = psum.tile([P, P], F32, name="gate_ps", tag="turned")
+        nc.tensor.transpose(gate_ps[:], gate_rows[:], ident[:])
+        gate_cols = keep.tile([P, D * CHUNKS], F32, name="gate_cols")
+        nc.scalar.activation(out=gate_cols[:], in_=gate_ps[:, 0 : D * CHUNKS], func=COPY)
+
+        w2w = keep.tile([P, 2 * N], U8, name="w2w", align_bytes=64)
+        nc.vector.tensor_copy(
+            out=w2w[:].rearrange("p (t m b) -> p t m b", t=PACK, b=2),
+            in_=w2w_raw[:].rearrange("p (m t b) -> p t m b", t=PACK, b=2),
+        )
+        raw10 = load_w1(1, 0, "stage2")
+
+        def gather_words(g, tag):
+            picked = keep.tile([P, S], U32, name="xw%d" % g, tag=tag, align_bytes=64)
+            nc.vector.tensor_copy(out=picked[:], in_=xw_table[g][:].bitcast(U32).indirect(offsets[:]))
+            return picked
+
+        xs = keep.tile([P, S], U8, name="xs", align_bytes=64)
+        nc.vector.tensor_copy(out=xs[:], in_=xs_table[:].indirect(offsets[:]))
+        xw = [gather_words(0, "xw0")]
+
+        w1w = [keep.tile([P, H], U32, name="w1w%d" % g, align_bytes=64) for g in range(PASSES)]
+        w1s = [keep.tile([P, H], U8, name="w1s%d" % g, align_bytes=64) for g in range(PASSES)]
+
+        def quantise_w1(g, h, raw, engine_copy):
+            grouped = keep.tile([P, PACK * HALF], BF16, name="grouped%d%d" % (g, h), tag="grouped%d%d" % (g, h), align_bytes=64)
+            round_and_interleave(engine_copy, grouped[:], raw[:])
+            for u in range(2):
+                cols = slice(u * HALF + h * P, u * HALF + (h + 1) * P)
+                nc.vector.quantize_mx(
+                    out=w1w[g][:, cols].bitcast(FP8X4),
+                    scales=w1s[g][:, cols],
+                    in_=grouped[:, u * K_PASS : (u + 1) * K_PASS],
+                )
+
+        quantise_w1(0, 0, raw00, [nc.scalar.copy])
+        raw11 = load_w1(1, 1, "stage3")
+        for q in range(QUADS):
+            nc.sync.dma_start(
+                out=w2s_raw[32 * q : 32 * q + 4, :].bitcast(I32),
+                in_=w2_scales[0, 4 * q : 4 * q + 4, :].bitcast(I32),
+            )
+
+        quantise_w1(0, 1, raw01, [nc.scalar.copy])
+        xw.append(gather_words(1, "grouped01"))
+        quantise_w1(1, 0, raw10, [nc.scalar.copy])
+        quantise_w1(1, 1, raw11, [nc.vector.tensor_copy, nc.scalar.copy])
+
+        w2s = keep.tile([P, N], U8, name="w2s", tag="grouped11", align_bytes=64)
+        nc.vector.tensor_copy(
+            out=w2s[:].rearrange("p (t m) -> p t m", t=PACK),
+            in_=w2s_raw[:].rearrange("p (m t) -> p t m", t=PACK),
+        )
+
+        out_rows = out_0.rearrange("(p t) v -> p t v", t=PACK)
+        out_words = out_1[0].rearrange("p n t -> p (n t)").bitcast(I32)
+        out_scales = keep.tile([P, V], U8, name="out_scales", align_bytes=64)
+        for c in range(CHUNKS):
+            feats = slice(c * P, (c + 1) * P)
+            y = []
+            for d in range(D):
+                bank = psum.tile([P, H], F32, name="y", tag="y", bufs=4)
+                cols = slice(d * V + c * P, d * V + (c + 1) * P)
+                for g in range(PASSES):
+                    nc.tensor.matmul_mx(
+                        out=bank[:],
+                        lhsT=xw[g][:, cols].bitcast(FP8X4),
+                        lhsT_scale=xs[4 * g :, cols],
+                        rhs=w1w[g][:].bitcast(FP8X4),
+                        rhs_scale=w1s[g][:],
+                        start=(g == 0),
+                        stop=(g == PASSES - 1),
+                    )
+                y.append(bank)
+            gated0 = ring.tile([P, H], F32, name="gated0")
+            nc.scalar.activation(out=gated0[:], in_=y[0][:], func=COPY, scale=gate_cols[:, c : c + 1])
+            zt = ring.tile([P, H], BF16, name="zt")
+            nc.vector.scalar_tensor_tensor(
+                out=zt[:], in0=y[1][:], scalar=gate_cols[:, CHUNKS + c : CHUNKS + c + 1], in1=gated0[:], op0=MULT, op1=ADD
+            )
+            turned = psum.tile([P, 2, P], F32, name="turned", tag="turned")
+            for u in range(2):
+                nc.tensor.transpose(turned[:, u, :], zt[:].bitcast(F32)[:, u * P : (u + 1) * P], ident[:])
+            z = ring.tile([P, PACK * P], BF16, name="z", align_bytes=64)
+            nc.scalar.copy(
+                out=z[:].bitcast(F32).rearrange("p (v u) -> p v u", u=2), in_=turned[:].rearrange("p u v -> p v u")
+            )
+            zw = ring.tile([P, P], U32, name="zw", align_bytes=64)
+            zs = ring.tile([P, P], U8, name="zs", align_bytes=64)
+            nc.vector.quantize_mx(out=zw[:].bitcast(FP8X4), scales=zs[:], in_=z[:])
+            acc = psum.tile([P, PACK, P], F32, name="acc", tag="acc")
+            for t in range(PACK):
+                nc.tensor.matmul_mx(
+                    out=acc[:, t, :],
+                    lhsT=w2w[:, 2 * P * t : 2 * P * (t + 1)].bitcast(FP4X4),
+                    lhsT_scale=w2s[:, P * t : P * (t + 1)],
+                    rhs=zw[:].bitcast(FP8X4),
+                    rhs_scale=zs[:],
+                    start=True,
+                    stop=True,
+                )
+            res = ring.tile([P, PACK, P], F32, name="res")
+            nc.scalar.copy(out=res[:], in_=acc[:])
+            nc.sync.dma_start(out=out_rows[:, :, feats], in_=res[:])
+            rounded = ring.tile([P, PACK * P], BF16, name="rounded", align_bytes=64)
+            nc.vector.tensor_copy(
+                out=rounded[:].rearrange("p (c i t) -> p c t i", i=4, t=PACK),
+                in_=res[:].rearrange("p t (c i) -> p c t i", i=4),
+            )
+            ow = ring.tile([P, P], U32, name="ow", align_bytes=64)
+            nc.vector.quantize_mx(out=ow[:].bitcast(FP8X4), scales=out_scales[:, feats], in_=rounded[:])
+            nc.sync.dma_start(out=out_words[:, feats], in_=ow[:].bitcast(I32))
+        for q, queue in enumerate((nc.sync, nc.scalar, nc.sync, nc.scalar)):
+            queue.dma_start(
+                out=out_2[0, 4 * q : 4 * q + 4, :].bitcast(I32), in_=out_scales[32 * q : 32 * q + 4, :].bitcast(I32)
+            )

@@ -43,7 +43,7 @@ def tile_picked_zbloom_none_po_kernel(
     with ExitStack() as ctx:
         keep = ctx.enter_context(tc.tile_pool(name="keep", bufs=1))
         ring = ctx.enter_context(tc.tile_pool(name="ring", bufs=4))
-        psum = ctx.enter_context(tc.psum_pool(name="psum", bufs=2))
+        psum = ctx.enter_context(tc.psum_pool(name="psum", bufs=1))
 
         offsets = keep.tile([P, S // 16], U16, name="offsets")
         nc.sync.dma_start(offsets[:], offs)
@@ -72,7 +72,7 @@ def tile_picked_zbloom_none_po_kernel(
             nc.sync.dma_start(out=raw[:], in_=w1_rows[g][:, :, h * HALF : (h + 1) * HALF])
             return raw
 
-        nc.sync.dma_start(
+        nc.scalar.dma_start(
             out=gate_rows[0 : D * CHUNKS, :], in_=gate[:, 0, :].rearrange("d (c p) -> d c p", p=P)
         )
         for q, queue in enumerate((nc.sync, nc.scalar, nc.sync, nc.scalar)):
@@ -85,7 +85,7 @@ def tile_picked_zbloom_none_po_kernel(
         raw01 = load_w1(0, 1, "stage1")
         load_x(1)
 
-        gate_ps = psum.tile([P, P], F32, name="gate_ps", tag="turned")
+        gate_ps = psum.tile([P, P], F32, name="gate_ps", tag="bank7")
         nc.tensor.transpose(gate_ps[:], gate_rows[:], ident[:])
         gate_cols = keep.tile([P, D * CHUNKS], F32, name="gate_cols")
         nc.scalar.activation(out=gate_cols[:], in_=gate_ps[:, 0 : D * CHUNKS], func=COPY)
@@ -142,11 +142,12 @@ def tile_picked_zbloom_none_po_kernel(
         out_rows = out_0.rearrange("(p t) v -> p t v", t=PACK)
         out_words = out_1[0].rearrange("p n t -> p (n t)").bitcast(I32)
         out_scales = keep.tile([P, V], U8, name="out_scales", align_bytes=64)
+        ow = keep.tile([P, V], U32, name="ow", align_bytes=64)
         for c in range(CHUNKS):
             feats = slice(c * P, (c + 1) * P)
             y = []
             for d in range(D):
-                bank = psum.tile([P, H], F32, name="y", tag="y", bufs=4)
+                bank = psum.tile([P, H], F32, name="y", tag="bank%d" % (D * c + d))
                 cols = slice(d * V + c * P, d * V + (c + 1) * P)
                 for g in range(PASSES):
                     nc.tensor.matmul_mx(
@@ -165,7 +166,7 @@ def tile_picked_zbloom_none_po_kernel(
             nc.vector.scalar_tensor_tensor(
                 out=zt[:], in0=y[1][:], scalar=gate_cols[:, CHUNKS + c : CHUNKS + c + 1], in1=gated0[:], op0=MULT, op1=ADD
             )
-            turned = psum.tile([P, 2, P], F32, name="turned", tag="turned")
+            turned = psum.tile([P, 2, P], F32, name="turned", tag="bank%d" % (D * c))
             for u in range(2):
                 nc.tensor.transpose(turned[:, u, :], zt[:].bitcast(F32)[:, u * P : (u + 1) * P], ident[:])
             z = ring.tile([P, PACK * P], BF16, name="z", align_bytes=64)
@@ -175,7 +176,7 @@ def tile_picked_zbloom_none_po_kernel(
             zw = ring.tile([P, P], U32, name="zw", align_bytes=64)
             zs = ring.tile([P, P], U8, name="zs", align_bytes=64)
             nc.vector.quantize_mx(out=zw[:].bitcast(FP8X4), scales=zs[:], in_=z[:])
-            acc = psum.tile([P, PACK, P], F32, name="acc", tag="acc")
+            acc = psum.tile([P, PACK, P], F32, name="acc", tag="bank%d" % (D * c + 1))
             for t in range(PACK):
                 nc.tensor.matmul_mx(
                     out=acc[:, t, :],
@@ -187,16 +188,17 @@ def tile_picked_zbloom_none_po_kernel(
                     stop=True,
                 )
             res = ring.tile([P, PACK, P], F32, name="res")
-            nc.scalar.copy(out=res[:], in_=acc[:])
+            (nc.vector.tensor_copy if c == 0 else nc.scalar.copy)(out=res[:], in_=acc[:])
             nc.sync.dma_start(out=out_rows[:, :, feats], in_=res[:])
             rounded = ring.tile([P, PACK * P], BF16, name="rounded", align_bytes=64)
             nc.vector.tensor_copy(
                 out=rounded[:].rearrange("p (c i t) -> p c t i", i=4, t=PACK),
                 in_=res[:].rearrange("p t (c i) -> p c t i", i=4),
             )
-            ow = ring.tile([P, P], U32, name="ow", align_bytes=64)
-            nc.vector.quantize_mx(out=ow[:].bitcast(FP8X4), scales=out_scales[:, feats], in_=rounded[:])
-            nc.sync.dma_start(out=out_words[:, feats], in_=ow[:].bitcast(I32))
+            nc.vector.quantize_mx(out=ow[:, feats].bitcast(FP8X4), scales=out_scales[:, feats], in_=rounded[:])
+            if c % 2 == 1:
+                pair = slice((c - 1) * P, (c + 1) * P)
+                nc.sync.dma_start(out=out_words[:, pair], in_=ow[:, pair].bitcast(I32))
         for q, queue in enumerate((nc.sync, nc.scalar, nc.sync, nc.scalar)):
             queue.dma_start(
                 out=out_2[0, 4 * q : 4 * q + 4, :].bitcast(I32), in_=out_scales[32 * q : 32 * q + 4, :].bitcast(I32)

@@ -82,8 +82,15 @@ def tile_picked_zbloom_none_po_kernel(
             )
         load_x(0)
         raw00 = load_w1(0, 0, "stage0")
-        raw01 = load_w1(0, 1, "stage1")
         load_x(1)
+        raw10 = load_w1(1, 0, "stage2")
+        raw01 = load_w1(0, 1, "stage1")
+        raw11 = load_w1(1, 1, "stage3")
+        for q in range(QUADS):
+            nc.sync.dma_start(
+                out=w2s_raw[32 * q : 32 * q + 4, :].bitcast(I32),
+                in_=w2_scales[0, 4 * q : 4 * q + 4, :].bitcast(I32),
+            )
 
         gate_ps = psum.tile([P, P], F32, name="gate_ps", tag="bank7")
         nc.tensor.transpose(gate_ps[:], gate_rows[:], ident[:])
@@ -95,7 +102,6 @@ def tile_picked_zbloom_none_po_kernel(
             out=w2w[:].rearrange("p (t m b) -> p t m b", t=PACK, b=2),
             in_=w2w_raw[:].rearrange("p (m t b) -> p t m b", t=PACK, b=2),
         )
-        raw10 = load_w1(1, 0, "stage2")
 
         def gather_words(g, tag):
             picked = keep.tile([P, S], U32, name="xw%d" % g, tag=tag, align_bytes=64)
@@ -106,32 +112,57 @@ def tile_picked_zbloom_none_po_kernel(
         nc.vector.tensor_copy(out=xs[:], in_=xs_table[:].indirect(offsets[:]))
         xw = [gather_words(0, "xw0")]
 
-        w1w = [keep.tile([P, H], U32, name="w1w%d" % g, align_bytes=64) for g in range(PASSES)]
-        w1s = [keep.tile([P, H], U8, name="w1s%d" % g, align_bytes=64) for g in range(PASSES)]
+        w1w, w1s = {}, {}
 
         def quantise_w1(g, h, raw, engine_copy):
-            grouped = keep.tile([P, PACK * HALF], BF16, name="grouped%d%d" % (g, h), tag="grouped%d%d" % (g, h), align_bytes=64)
+            grouped = keep.tile([P, PACK * HALF], BF16, name="grouped%d%d" % (g, h), align_bytes=64)
             round_and_interleave(engine_copy, grouped[:], raw[:])
-            for u in range(2):
-                cols = slice(u * HALF + h * P, u * HALF + (h + 1) * P)
-                nc.vector.quantize_mx(
-                    out=w1w[g][:, cols].bitcast(FP8X4),
-                    scales=w1s[g][:, cols],
-                    in_=grouped[:, u * K_PASS : (u + 1) * K_PASS],
-                )
+            w1w[g, h] = keep.tile([P, HALF], U32, name="w1w%d%d" % (g, h), align_bytes=64)
+            w1s[g, h] = keep.tile([P, HALF], U8, name="w1s%d%d" % (g, h), align_bytes=64)
+            nc.vector.quantize_mx(out=w1w[g, h][:].bitcast(FP8X4), scales=w1s[g, h][:], in_=grouped[:])
 
         quantise_w1(0, 0, raw00, [nc.scalar.copy])
-        raw11 = load_w1(1, 1, "stage3")
-        for q in range(QUADS):
-            nc.sync.dma_start(
-                out=w2s_raw[32 * q : 32 * q + 4, :].bitcast(I32),
-                in_=w2_scales[0, 4 * q : 4 * q + 4, :].bitcast(I32),
+        xw.append(gather_words(1, "grouped00"))
+
+        y = {}
+        zt = [keep.tile([P, H], BF16, name="zt%d" % c) for c in range(CHUNKS)]
+
+        def first_product(c, d, g, h):
+            cols = slice(d * V + c * P, d * V + (c + 1) * P)
+            nc.tensor.matmul_mx(
+                out=y[c, d][:, h * HALF : (h + 1) * HALF],
+                lhsT=xw[g][:, cols].bitcast(FP8X4),
+                lhsT_scale=xs[4 * g :, cols],
+                rhs=w1w[g, h][:].bitcast(FP8X4),
+                rhs_scale=w1s[g, h][:],
+                start=(g == 0),
+                stop=(g == PASSES - 1),
             )
 
-        quantise_w1(0, 1, raw01, [nc.scalar.copy])
-        xw.append(gather_words(1, "grouped01"))
+        def weigh(c, h):
+            half = slice(h * HALF, (h + 1) * HALF)
+            gated0 = ring.tile([P, HALF], F32, name="gated0")
+            nc.scalar.activation(out=gated0[:], in_=y[c, 0][:, half], func=COPY, scale=gate_cols[:, c : c + 1])
+            nc.vector.scalar_tensor_tensor(
+                out=zt[c][:].rearrange("p (u h x) -> p h u x", u=2, h=2)[:, h],
+                in0=y[c, 1][:, half].rearrange("p (u x) -> p u x", u=2),
+                scalar=gate_cols[:, CHUNKS + c : CHUNKS + c + 1],
+                in1=gated0[:].rearrange("p (u x) -> p u x", u=2),
+                op0=MULT,
+                op1=ADD,
+            )
+
+        for c in range(CHUNKS):
+            for d in range(D):
+                y[c, d] = psum.tile([P, H], F32, name="y", tag="bank%d" % (D * c + d))
+                first_product(c, d, 0, 0)
         quantise_w1(1, 0, raw10, [nc.scalar.copy])
-        quantise_w1(1, 1, raw11, [nc.vector.tensor_copy, nc.scalar.copy])
+        quantise_w1(0, 1, raw01, [nc.scalar.copy])
+        quantise_w1(1, 1, raw11, [nc.vector.tensor_copy])
+        for c in range(CHUNKS):
+            for d in range(D):
+                first_product(c, d, 1, 0)
+            weigh(c, 0)
 
         w2s = keep.tile([P, N], U8, name="w2s", tag="grouped11", align_bytes=64)
         nc.vector.tensor_copy(
@@ -143,43 +174,33 @@ def tile_picked_zbloom_none_po_kernel(
         out_words = out_1[0].rearrange("p n t -> p (n t)").bitcast(I32)
         out_scales = keep.tile([P, V], U8, name="out_scales", align_bytes=64)
         ow = keep.tile([P, V], U32, name="ow", align_bytes=64)
-        for c in range(CHUNKS):
-            feats = slice(c * P, (c + 1) * P)
-            y = []
+        acc = {}
+
+        def finish_first(c):
             for d in range(D):
-                bank = psum.tile([P, H], F32, name="y", tag="bank%d" % (D * c + d))
-                cols = slice(d * V + c * P, d * V + (c + 1) * P)
                 for g in range(PASSES):
-                    nc.tensor.matmul_mx(
-                        out=bank[:],
-                        lhsT=xw[g][:, cols].bitcast(FP8X4),
-                        lhsT_scale=xs[4 * g :, cols],
-                        rhs=w1w[g][:].bitcast(FP8X4),
-                        rhs_scale=w1s[g][:],
-                        start=(g == 0),
-                        stop=(g == PASSES - 1),
-                    )
-                y.append(bank)
-            gated0 = ring.tile([P, H], F32, name="gated0")
-            nc.scalar.activation(out=gated0[:], in_=y[0][:], func=COPY, scale=gate_cols[:, c : c + 1])
-            zt = ring.tile([P, H], BF16, name="zt")
-            nc.vector.scalar_tensor_tensor(
-                out=zt[:], in0=y[1][:], scalar=gate_cols[:, CHUNKS + c : CHUNKS + c + 1], in1=gated0[:], op0=MULT, op1=ADD
-            )
+                    first_product(c, d, g, 1)
+            weigh(c, 1)
+
+        z = {}
+
+        def turn(c):
             turned = psum.tile([P, 2, P], F32, name="turned", tag="bank%d" % (D * c))
             for u in range(2):
-                nc.tensor.transpose(turned[:, u, :], zt[:].bitcast(F32)[:, u * P : (u + 1) * P], ident[:])
-            z = ring.tile([P, PACK * P], BF16, name="z", align_bytes=64)
+                nc.tensor.transpose(turned[:, u, :], zt[c][:].bitcast(F32)[:, u * P : (u + 1) * P], ident[:])
+            z[c] = ring.tile([P, PACK * P], BF16, name="z", align_bytes=64)
             nc.scalar.copy(
-                out=z[:].bitcast(F32).rearrange("p (v u) -> p v u", u=2), in_=turned[:].rearrange("p u v -> p v u")
+                out=z[c][:].bitcast(F32).rearrange("p (v u) -> p v u", u=2), in_=turned[:].rearrange("p u v -> p v u")
             )
+
+        def second_product(c):
             zw = ring.tile([P, P], U32, name="zw", align_bytes=64)
             zs = ring.tile([P, P], U8, name="zs", align_bytes=64)
-            nc.vector.quantize_mx(out=zw[:].bitcast(FP8X4), scales=zs[:], in_=z[:])
-            acc = psum.tile([P, PACK, P], F32, name="acc", tag="bank%d" % (D * c + 1))
+            nc.vector.quantize_mx(out=zw[:].bitcast(FP8X4), scales=zs[:], in_=z[c][:])
+            acc[c] = psum.tile([P, PACK, P], F32, name="acc", tag="bank%d" % (D * c + 1))
             for t in range(PACK):
                 nc.tensor.matmul_mx(
-                    out=acc[:, t, :],
+                    out=acc[c][:, t, :],
                     lhsT=w2w[:, 2 * P * t : 2 * P * (t + 1)].bitcast(FP4X4),
                     lhsT_scale=w2s[:, P * t : P * (t + 1)],
                     rhs=zw[:].bitcast(FP8X4),
@@ -187,8 +208,11 @@ def tile_picked_zbloom_none_po_kernel(
                     start=True,
                     stop=True,
                 )
+
+        def hand_out(c):
+            feats = slice(c * P, (c + 1) * P)
             res = ring.tile([P, PACK, P], F32, name="res")
-            (nc.vector.tensor_copy if c == 0 else nc.scalar.copy)(out=res[:], in_=acc[:])
+            (nc.vector.tensor_copy if c == 0 else nc.scalar.copy)(out=res[:], in_=acc[c][:])
             nc.sync.dma_start(out=out_rows[:, :, feats], in_=res[:])
             rounded = ring.tile([P, PACK * P], BF16, name="rounded", align_bytes=64)
             nc.vector.tensor_copy(
@@ -199,6 +223,10 @@ def tile_picked_zbloom_none_po_kernel(
             if c % 2 == 1:
                 pair = slice((c - 1) * P, (c + 1) * P)
                 nc.sync.dma_start(out=out_words[:, pair], in_=ow[:, pair].bitcast(I32))
+
+        for stage in (finish_first, turn, second_product, hand_out):
+            for c in range(CHUNKS):
+                stage(c)
         for q, queue in enumerate((nc.sync, nc.scalar, nc.sync, nc.scalar)):
             queue.dma_start(
                 out=out_2[0, 4 * q : 4 * q + 4, :].bitcast(I32), in_=out_scales[32 * q : 32 * q + 4, :].bitcast(I32)

@@ -174,7 +174,8 @@ def tile_picked_zbloom_none_po_kernel(
         out_words = out_1[0].rearrange("p n t -> p (n t)").bitcast(I32)
         out_scales = keep.tile([P, V], U8, name="out_scales", align_bytes=64)
         ow = keep.tile([P, V], U32, name="ow", align_bytes=64)
-        acc = {}
+        acc, results = {}, {}
+        res = [keep.tile([P, PACK, 2 * P], F32, name="res%d" % n) for n in range(2)]
 
         def finish_first(c):
             for d in range(D):
@@ -210,23 +211,41 @@ def tile_picked_zbloom_none_po_kernel(
                 )
 
         def hand_out(c):
-            feats = slice(c * P, (c + 1) * P)
-            res = ring.tile([P, PACK, P], F32, name="res")
-            (nc.vector.tensor_copy if c == 0 else nc.scalar.copy)(out=res[:], in_=acc[c][:])
-            nc.sync.dma_start(out=out_rows[:, :, feats], in_=res[:])
-            rounded = ring.tile([P, PACK * P], BF16, name="rounded", align_bytes=64)
-            nc.vector.tensor_copy(
-                out=rounded[:].rearrange("p (c i t) -> p c t i", i=4, t=PACK),
-                in_=res[:].rearrange("p t (c i) -> p c t i", i=4),
-            )
-            nc.vector.quantize_mx(out=ow[:, feats].bitcast(FP8X4), scales=out_scales[:, feats], in_=rounded[:])
+            results[c] = res[c // 2][:, :, (c % 2) * P : (c % 2 + 1) * P]
+            (nc.vector.tensor_copy if c == 0 else nc.scalar.copy)(out=results[c], in_=acc[c][:])
             if c % 2 == 1:
-                pair = slice((c - 1) * P, (c + 1) * P)
-                nc.sync.dma_start(out=out_words[:, pair], in_=ow[:, pair].bitcast(I32))
+                nc.sync.dma_start(out=out_rows[:, :, (c - 1) * P : (c + 1) * P], in_=res[c // 2][:])
+
+        rounded = keep.tile([P, CHUNKS * PACK * P], BF16, name="rounded", align_bytes=64)
+
+        def round_result(c):
+            nc.vector.tensor_copy(
+                out=rounded[:, c * K_PASS : (c + 1) * K_PASS].rearrange("p (c i t) -> p c t i", i=4, t=PACK),
+                in_=results[c].rearrange("p t (c i) -> p c t i", i=4),
+            )
+
+        def quantise_result(first, end):
+            feats = slice(first * P, end * P)
+            nc.vector.quantize_mx(
+                out=ow[:, feats].bitcast(FP8X4),
+                scales=out_scales[:, feats],
+                in_=rounded[:, first * K_PASS : end * K_PASS],
+            )
+
+        def store_words(first, end):
+            feats = slice(first * P, end * P)
+            nc.sync.dma_start(out=out_words[:, feats], in_=ow[:, feats].bitcast(I32))
 
         for stage in (finish_first, turn, second_product, hand_out):
             for c in range(CHUNKS):
                 stage(c)
+        for c in (1, 0, 2, 3):
+            round_result(c)
+        quantise_result(0, 2)
+        store_words(0, 2)
+        quantise_result(2, 3)
+        quantise_result(3, 4)
+        store_words(2, 4)
         for q, queue in enumerate((nc.sync, nc.scalar, nc.sync, nc.scalar)):
             queue.dma_start(
                 out=out_2[0, 4 * q : 4 * q + 4, :].bitcast(I32), in_=out_scales[32 * q : 32 * q + 4, :].bitcast(I32)

@@ -141,7 +141,7 @@ def tile_picked_zbloom_none_po_kernel(
 
         def weigh(c, h):
             half = slice(h * HALF, (h + 1) * HALF)
-            gated0 = ring.tile([P, HALF], F32, name="gated0")
+            gated0 = keep.tile([P, HALF], F32, name="gated%d%d" % (c, h), align_bytes=64)
             nc.scalar.activation(out=gated0[:], in_=y[c, 0][:, half], func=COPY, scale=gate_cols[:, c : c + 1])
             nc.vector.scalar_tensor_tensor(
                 out=zt[c][:].rearrange("p (u h x) -> p h u x", u=2, h=2)[:, h],
@@ -163,12 +163,6 @@ def tile_picked_zbloom_none_po_kernel(
             for d in range(D):
                 first_product(c, d, 1, 0)
             weigh(c, 0)
-
-        w2s = keep.tile([P, N], U8, name="w2s", tag="grouped11", align_bytes=64)
-        nc.vector.tensor_copy(
-            out=w2s[:].rearrange("p (t m) -> p t m", t=PACK),
-            in_=w2s_raw[:].rearrange("p (m t) -> p t m", t=PACK),
-        )
 
         out_rows = out_0.rearrange("(p t) v -> p t v", t=PACK)
         out_words = out_1[0].rearrange("p n t -> p (n t)").bitcast(I32)
@@ -236,17 +230,24 @@ def tile_picked_zbloom_none_po_kernel(
             feats = slice(first * P, end * P)
             nc.sync.dma_start(out=out_words[:, feats], in_=ow[:, feats].bitcast(I32))
 
-        for stage in (finish_first, turn, second_product, hand_out):
+        for c in range(CHUNKS):
+            finish_first(c)
+        w2s = keep.tile([P, N], U8, name="w2s", tag="gated11", align_bytes=64)
+        nc.vector.tensor_copy(
+            out=w2s[:].rearrange("p (t m) -> p t m", t=PACK),
+            in_=w2s_raw[:].rearrange("p (m t) -> p t m", t=PACK),
+        )
+
+        for stage in (turn, second_product, hand_out):
             for c in range(CHUNKS):
                 stage(c)
         for c in (1, 0, 2, 3):
             round_result(c)
         quantise_result(0, 2)
-        store_words(0, 2)
         quantise_result(2, 3)
         quantise_result(3, 4)
-        store_words(2, 4)
-        for q, queue in enumerate((nc.sync, nc.scalar, nc.sync, nc.scalar)):
-            queue.dma_start(
+        store_words(0, 4)
+        for q in range(QUADS):
+            nc.scalar.dma_start(
                 out=out_2[0, 4 * q : 4 * q + 4, :].bitcast(I32), in_=out_scales[32 * q : 32 * q + 4, :].bitcast(I32)
             )

@@ -206,7 +206,7 @@ def tile_picked_zbloom_none_po_kernel(
 
         def hand_out(c):
             results[c] = res[c // 2][:, :, (c % 2) * P : (c % 2 + 1) * P]
-            (nc.vector.tensor_copy if c == 0 else nc.scalar.copy)(out=results[c], in_=acc[c][:])
+            (nc.vector.tensor_copy if c == 1 else nc.scalar.copy)(out=results[c], in_=acc[c][:])
             if c % 2 == 1:
                 nc.sync.dma_start(out=out_rows[:, :, (c - 1) * P : (c + 1) * P], in_=res[c // 2][:])
 
@@ -241,7 +241,7 @@ def tile_picked_zbloom_none_po_kernel(
         for stage in (turn, second_product, hand_out):
             for c in range(CHUNKS):
                 stage(c)
-        for c in (1, 0, 2, 3):
+        for c in range(CHUNKS):
             round_result(c)
         quantise_result(0, 2)
         quantise_result(2, 3)

@@ -49,17 +49,21 @@ def tile_picked_zbloom_none_po_kernel(
         nc.sync.dma_start(offsets[:], offs)
 
         xs_table = keep.tile([P, T], U8, name="xs_table", align_bytes=64)
-        nc.vector.memset(xs_table[:].bitcast(I32), 0)
-        gate_rows = keep.tile([P, P], F32, name="gate_rows")
-        nc.gpsimd.memset(gate_rows[:], 0.0)
-
+        for g, queue in enumerate((nc.sync, nc.sync)):
+            queue.dma_start(out=xs_table[g:32:PASSES, :].bitcast(I32), in_=x_scales[g].bitcast(I32))
         ident = keep.tile([P, P], F32, name="ident")
         make_identity(nc, ident[:])
-        w2s_raw = keep.tile([P, N], U8, name="w2s_raw", align_bytes=64)
-        nc.gpsimd.memset(w2s_raw[:].bitcast(I32), 0)
+        gate_rows = keep.tile([P, P], F32, name="gate_rows")
+        blank = keep.tile([P, 8], F32, name="blank")
+        nc.vector.memset(blank[:], 0.0)
+        nc.scalar.activation(out=gate_rows[:], in_=blank[:, 0:1].to_broadcast([P, P]), func=COPY)
+        nc.vector.memset(xs_table[32:64, :].bitcast(I32), 0)
+        nc.vector.memset(xs_table[64:128, :].bitcast(I32), 0)
+        xs = keep.tile([P, PASSES * S], U8, name="xs", align_bytes=64)
+        nc.gpsimd.memset(xs[:].bitcast(I32), 0)
 
-        w2w_raw = keep.tile([P, 2 * N], U8, name="w2w_raw")
-        nc.sync.dma_start(out=w2w_raw[:].bitcast(I32), in_=w2_words[0].bitcast(I32))
+        w2w_raw = keep.tile([P, 2 * N], U8, name="w2w_raw", align_bytes=64)
+        nc.scalar.dma_start(out=w2w_raw[:].bitcast(I32), in_=w2_words[0].bitcast(I32))
 
         xw_table = [keep.tile([P, T], I32, name="xw_table%d" % g, align_bytes=64) for g in range(PASSES)]
         w1_rows = [w1[g * K_PASS : (g + 1) * K_PASS, :].rearrange("(p j) c -> p j c", j=PACK) for g in range(PASSES)]
@@ -68,61 +72,66 @@ def tile_picked_zbloom_none_po_kernel(
             nc.sync.dma_start(out=xw_table[g][:], in_=x_words[g].rearrange("p n t -> p (n t)").bitcast(I32))
 
         def load_w1(g, h, tag):
-            raw = keep.tile([P, PACK, HALF], F32, name="w1_raw%d%d" % (g, h), tag=tag)
+            raw = keep.tile([P, PACK, HALF], F32, name="w1_raw%d%d" % (g, h), tag=tag, align_bytes=64)
             nc.sync.dma_start(out=raw[:], in_=w1_rows[g][:, :, h * HALF : (h + 1) * HALF])
-            return raw
+            return raw[:]
 
         nc.scalar.dma_start(
             out=gate_rows[0 : D * CHUNKS, :], in_=gate[:, 0, :].rearrange("d (c p) -> d c p", p=P)
         )
-        for q, queue in enumerate((nc.sync, nc.scalar, nc.sync, nc.scalar)):
-            queue.dma_start(
-                out=xs_table[32 * q : 32 * q + 4 * PASSES, :].bitcast(I32),
-                in_=x_scales[:, 4 * q : 4 * q + 4, :].bitcast(I32),
-            )
         load_x(0)
         raw00 = load_w1(0, 0, "stage0")
         load_x(1)
-        raw10 = load_w1(1, 0, "stage2")
-        raw01 = load_w1(0, 1, "stage1")
-        raw11 = load_w1(1, 1, "stage3")
+
+        xs_picked = keep.tile([P, S], U8, name="xs_picked", align_bytes=64)
+        nc.vector.tensor_copy(out=xs_picked[:], in_=xs_table[:].indirect(offsets[:]))
         for q in range(QUADS):
-            nc.sync.dma_start(
-                out=w2s_raw[32 * q : 32 * q + 4, :].bitcast(I32),
-                in_=w2_scales[0, 4 * q : 4 * q + 4, :].bitcast(I32),
+            nc.scalar.dma_start(
+                out=xs[32 * q : 32 * q + 4, :].bitcast(I32),
+                in_=xs_picked[8 * q : 8 * q + 8, :].bitcast(I32),
             )
-
-        gate_ps = psum.tile([P, P], F32, name="gate_ps", tag="bank7")
-        nc.tensor.transpose(gate_ps[:], gate_rows[:], ident[:])
-        gate_cols = keep.tile([P, D * CHUNKS], F32, name="gate_cols")
-        nc.scalar.activation(out=gate_cols[:], in_=gate_ps[:, 0 : D * CHUNKS], func=COPY)
-
-        w2w = keep.tile([P, 2 * N], U8, name="w2w", align_bytes=64)
-        nc.vector.tensor_copy(
-            out=w2w[:].rearrange("p (t m b) -> p t m b", t=PACK, b=2),
-            in_=w2w_raw[:].rearrange("p (m t b) -> p t m b", t=PACK, b=2),
-        )
 
         def gather_words(g, tag):
             picked = keep.tile([P, S], U32, name="xw%d" % g, tag=tag, align_bytes=64)
             nc.vector.tensor_copy(out=picked[:], in_=xw_table[g][:].bitcast(U32).indirect(offsets[:]))
             return picked
 
-        xs = keep.tile([P, S], U8, name="xs", align_bytes=64)
-        nc.vector.tensor_copy(out=xs[:], in_=xs_table[:].indirect(offsets[:]))
         xw = [gather_words(0, "xw0")]
+        raw10 = load_w1(1, 0, "xs_table")
+        gate_ps = psum.tile([P, P], F32, name="gate_ps", tag="bank7")
+        nc.tensor.transpose(gate_ps[:], gate_rows[:], ident[:])
+        gate_cols = keep.tile([P, D * CHUNKS], F32, name="gate_cols")
+        nc.scalar.activation(out=gate_cols[:], in_=gate_ps[:, 0 : D * CHUNKS], func=COPY)
+
 
         w1w, w1s = {}, {}
 
         def quantise_w1(g, h, raw, engine_copy):
             grouped = keep.tile([P, PACK * HALF], BF16, name="grouped%d%d" % (g, h), align_bytes=64)
-            round_and_interleave(engine_copy, grouped[:], raw[:])
+            round_and_interleave(engine_copy, grouped[:], raw)
             w1w[g, h] = keep.tile([P, HALF], U32, name="w1w%d%d" % (g, h), align_bytes=64)
             w1s[g, h] = keep.tile([P, HALF], U8, name="w1s%d%d" % (g, h), align_bytes=64)
             nc.vector.quantize_mx(out=w1w[g, h][:].bitcast(FP8X4), scales=w1s[g, h][:], in_=grouped[:])
 
         quantise_w1(0, 0, raw00, [nc.scalar.copy])
-        xw.append(gather_words(1, "grouped00"))
+        late = keep.tile([P, PASSES, PACK, HALF], F32, name="late", tag="stage0", align_bytes=64)
+        for g in range(PASSES):
+            nc.sync.dma_start(out=late[:, g], in_=w1_rows[g][:, :, HALF:])
+        raw01, raw11 = late[:, 0], late[:, 1]
+        w2s_raw = keep.tile([P, N], U8, name="w2s_raw", tag="xw_table0", align_bytes=64)
+        nc.gpsimd.memset(w2s_raw[:].bitcast(I32), 0)
+        for q in range(QUADS):
+            nc.sync.dma_start(
+                out=w2s_raw[32 * q : 32 * q + 4, :].bitcast(I32),
+                in_=w2_scales[0, 4 * q : 4 * q + 4, :].bitcast(I32),
+            )
+
+        w2w = keep.tile([P, 2 * N], U8, name="w2w", tag="grouped00", align_bytes=64)
+        nc.vector.tensor_copy(
+            out=w2w[:].rearrange("p (t m b) -> p t m b", t=PACK, b=2),
+            in_=w2w_raw[:].rearrange("p (m t b) -> p t m b", t=PACK, b=2),
+        )
+        xw.append(gather_words(1, "w2w_raw"))
 
         y = {}
         zt = [keep.tile([P, H], BF16, name="zt%d" % c) for c in range(CHUNKS)]
@@ -132,7 +141,7 @@ def tile_picked_zbloom_none_po_kernel(
             nc.tensor.matmul_mx(
                 out=y[c, d][:, h * HALF : (h + 1) * HALF],
                 lhsT=xw[g][:, cols].bitcast(FP8X4),
-                lhsT_scale=xs[4 * g :, cols],
+                lhsT_scale=xs[:, g * S + d * V + c * P : g * S + d * V + (c + 1) * P],
                 rhs=w1w[g, h][:].bitcast(FP8X4),
                 rhs_scale=w1s[g, h][:],
                 start=(g == 0),

@@ -65,6 +65,12 @@ def tile_picked_zbloom_none_po_kernel(
         w2w_raw = keep.tile([P, 2 * N], U8, name="w2w_raw", align_bytes=64)
         nc.scalar.dma_start(out=w2w_raw[:].bitcast(I32), in_=w2_words[0].bitcast(I32))
 
+        w2w = keep.tile([P, 2 * N], U8, name="w2w", align_bytes=64)
+        nc.gpsimd.tensor_copy(
+            out=w2w[:].rearrange("p (t m b) -> p t m b", t=PACK, b=2),
+            in_=w2w_raw[:].rearrange("p (m t b) -> p t m b", t=PACK, b=2),
+        )
+
         xw_table = [keep.tile([P, T], I32, name="xw_table%d" % g, align_bytes=64) for g in range(PASSES)]
         w1_rows = [w1[g * K_PASS : (g + 1) * K_PASS, :].rearrange("(p j) c -> p j c", j=PACK) for g in range(PASSES)]
 
@@ -126,12 +132,7 @@ def tile_picked_zbloom_none_po_kernel(
                 in_=w2_scales[0, 4 * q : 4 * q + 4, :].bitcast(I32),
             )
 
-        w2w = keep.tile([P, 2 * N], U8, name="w2w", tag="grouped00", align_bytes=64)
-        nc.vector.tensor_copy(
-            out=w2w[:].rearrange("p (t m b) -> p t m b", t=PACK, b=2),
-            in_=w2w_raw[:].rearrange("p (m t b) -> p t m b", t=PACK, b=2),
-        )
-        xw.append(gather_words(1, "w2w_raw"))
+        xw.append(gather_words(1, "grouped00"))
 
         y = {}
         zt = [keep.tile([P, H], BF16, name="zt%d" % c) for c in range(CHUNKS)]
@@ -241,8 +242,8 @@ def tile_picked_zbloom_none_po_kernel(
 
         for c in range(CHUNKS):
             finish_first(c)
-        w2s = keep.tile([P, N], U8, name="w2s", tag="gated11", align_bytes=64)
-        nc.vector.tensor_copy(
+        w2s = keep.tile([P, N], U8, name="w2s", tag="grouped11", align_bytes=64)
+        nc.gpsimd.tensor_copy(
             out=w2s[:].rearrange("p (t m) -> p t m", t=PACK),
             in_=w2s_raw[:].rearrange("p (m t) -> p t m", t=PACK),
         )

@@ -42,7 +42,6 @@ def tile_picked_zbloom_none_po_kernel(
     nc = tc.nc
     with ExitStack() as ctx:
         keep = ctx.enter_context(tc.tile_pool(name="keep", bufs=1))
-        ring = ctx.enter_context(tc.tile_pool(name="ring", bufs=4))
         psum = ctx.enter_context(tc.psum_pool(name="psum", bufs=1))
 
         offsets = keep.tile([P, S // 16], U16, name="offsets")
@@ -51,16 +50,15 @@ def tile_picked_zbloom_none_po_kernel(
         xs_table = keep.tile([P, T], U8, name="xs_table", align_bytes=64)
         for g, queue in enumerate((nc.sync, nc.sync)):
             queue.dma_start(out=xs_table[g:32:PASSES, :].bitcast(I32), in_=x_scales[g].bitcast(I32))
+        gate_rows = keep.tile([P, P], F32, name="gate_rows", align_bytes=64)
+        nc.gpsimd.memset(gate_rows[:], 0.0)
+        nc.sync.dma_start(
+            out=gate_rows[0 : D * CHUNKS, :], in_=gate[:, 0, :].rearrange("d (c p) -> d c p", p=P)
+        )
         ident = keep.tile([P, P], F32, name="ident")
         make_identity(nc, ident[:])
-        gate_rows = keep.tile([P, P], F32, name="gate_rows")
-        blank = keep.tile([P, 8], F32, name="blank")
-        nc.vector.memset(blank[:], 0.0)
-        nc.scalar.activation(out=gate_rows[:], in_=blank[:, 0:1].to_broadcast([P, P]), func=COPY)
         nc.vector.memset(xs_table[32:64, :].bitcast(I32), 0)
         nc.vector.memset(xs_table[64:128, :].bitcast(I32), 0)
-        xs = keep.tile([P, PASSES * S], U8, name="xs", align_bytes=64)
-        nc.gpsimd.memset(xs[:].bitcast(I32), 0)
 
         w2w_raw = keep.tile([P, 2 * N], U8, name="w2w_raw", align_bytes=64)
         nc.scalar.dma_start(out=w2w_raw[:].bitcast(I32), in_=w2_words[0].bitcast(I32))
@@ -82,9 +80,13 @@ def tile_picked_zbloom_none_po_kernel(
             nc.sync.dma_start(out=raw[:], in_=w1_rows[g][:, :, h * HALF : (h + 1) * HALF])
             return raw[:]
 
-        nc.scalar.dma_start(
-            out=gate_rows[0 : D * CHUNKS, :], in_=gate[:, 0, :].rearrange("d (c p) -> d c p", p=P)
-        )
+        gate_ps = psum.tile([P, P], F32, name="gate_ps", tag="bank7")
+        nc.tensor.transpose(gate_ps[:], gate_rows[:], ident[:])
+        gate_cols = keep.tile([P, D * CHUNKS], F32, name="gate_cols")
+        nc.scalar.activation(out=gate_cols[:], in_=gate_ps[:, 0 : D * CHUNKS], func=COPY)
+        xs = keep.tile([P, PASSES * S], U8, name="xs", tag="gate_rows", align_bytes=64)
+        nc.gpsimd.memset(xs[:].bitcast(I32), 0)
+
         load_x(0)
         raw00 = load_w1(0, 0, "stage0")
         load_x(1)
@@ -104,11 +106,6 @@ def tile_picked_zbloom_none_po_kernel(
 
         xw = [gather_words(0, "xw0")]
         raw10 = load_w1(1, 0, "xs_table")
-        gate_ps = psum.tile([P, P], F32, name="gate_ps", tag="bank7")
-        nc.tensor.transpose(gate_ps[:], gate_rows[:], ident[:])
-        gate_cols = keep.tile([P, D * CHUNKS], F32, name="gate_cols")
-        nc.scalar.activation(out=gate_cols[:], in_=gate_ps[:, 0 : D * CHUNKS], func=COPY)
-
 
         w1w, w1s = {}, {}
 
@@ -124,14 +121,6 @@ def tile_picked_zbloom_none_po_kernel(
         for g in range(PASSES):
             nc.sync.dma_start(out=late[:, g], in_=w1_rows[g][:, :, HALF:])
         raw01, raw11 = late[:, 0], late[:, 1]
-        w2s_raw = keep.tile([P, N], U8, name="w2s_raw", tag="xw_table0", align_bytes=64)
-        nc.gpsimd.memset(w2s_raw[:].bitcast(I32), 0)
-        for q in range(QUADS):
-            nc.sync.dma_start(
-                out=w2s_raw[32 * q : 32 * q + 4, :].bitcast(I32),
-                in_=w2_scales[0, 4 * q : 4 * q + 4, :].bitcast(I32),
-            )
-
         xw.append(gather_words(1, "grouped00"))
 
         y = {}
@@ -162,11 +151,30 @@ def tile_picked_zbloom_none_po_kernel(
                 op1=ADD,
             )
 
+        unread = psum.tile([P, H], F32, name="unread", tag="bank7")
+        for n in range(4):
+            nc.tensor.matmul_mx(
+                out=unread[:],
+                lhsT=xw[0][:, 0:P].bitcast(FP8X4),
+                lhsT_scale=xs_picked[:, 0:P],
+                rhs=xw[0][:, 0:H].bitcast(FP8X4),
+                rhs_scale=xs_picked[:, 0:H],
+                start=True,
+                stop=True,
+            )
         for c in range(CHUNKS):
             for d in range(D):
                 y[c, d] = psum.tile([P, H], F32, name="y", tag="bank%d" % (D * c + d))
                 first_product(c, d, 0, 0)
         quantise_w1(1, 0, raw10, [nc.scalar.copy])
+        w2s_raw = keep.tile([P, N], U8, name="w2s_raw", tag="xs_table", align_bytes=64)
+        nc.gpsimd.memset(w2s_raw[:].bitcast(I32), 0)
+        for q in range(QUADS):
+            nc.sync.dma_start(
+                out=w2s_raw[32 * q : 32 * q + 4, :].bitcast(I32),
+                in_=w2_scales[0, 4 * q : 4 * q + 4, :].bitcast(I32),
+            )
+
         quantise_w1(0, 1, raw01, [nc.scalar.copy])
         quantise_w1(1, 1, raw11, [nc.vector.tensor_copy])
         for c in range(CHUNKS):
@@ -178,7 +186,6 @@ def tile_picked_zbloom_none_po_kernel(
         out_words = out_1[0].rearrange("p n t -> p (n t)").bitcast(I32)
         out_scales = keep.tile([P, V], U8, name="out_scales", align_bytes=64)
         ow = keep.tile([P, V], U32, name="ow", align_bytes=64)
-        acc, results = {}, {}
         res = [keep.tile([P, PACK, 2 * P], F32, name="res%d" % n) for n in range(2)]
 
         def finish_first(c):
@@ -187,45 +194,59 @@ def tile_picked_zbloom_none_po_kernel(
                     first_product(c, d, g, 1)
             weigh(c, 1)
 
-        z = {}
+        z = [keep.tile([P, PACK * P], BF16, name="z%d" % c, align_bytes=64) for c in range(CHUNKS)]
 
         def turn(c):
             turned = psum.tile([P, 2, P], F32, name="turned", tag="bank%d" % (D * c))
             for u in range(2):
                 nc.tensor.transpose(turned[:, u, :], zt[c][:].bitcast(F32)[:, u * P : (u + 1) * P], ident[:])
-            z[c] = ring.tile([P, PACK * P], BF16, name="z", align_bytes=64)
             nc.scalar.copy(
-                out=z[c][:].bitcast(F32).rearrange("p (v u) -> p v u", u=2), in_=turned[:].rearrange("p u v -> p v u")
+                out=z[c][:].bitcast(F32).rearrange("p (v u) -> p v u", u=2),
+                in_=turned[:].rearrange("p u v -> p v u"),
             )
 
-        def second_product(c):
-            zw = ring.tile([P, P], U32, name="zw", align_bytes=64)
-            zs = ring.tile([P, P], U8, name="zs", align_bytes=64)
-            nc.vector.quantize_mx(out=zw[:].bitcast(FP8X4), scales=zs[:], in_=z[c][:])
-            acc[c] = psum.tile([P, PACK, P], F32, name="acc", tag="bank%d" % (D * c + 1))
-            for t in range(PACK):
-                nc.tensor.matmul_mx(
-                    out=acc[c][:, t, :],
-                    lhsT=w2w[:, 2 * P * t : 2 * P * (t + 1)].bitcast(FP4X4),
-                    lhsT_scale=w2s[:, P * t : P * (t + 1)],
-                    rhs=zw[:].bitcast(FP8X4),
-                    rhs_scale=zs[:],
-                    start=True,
-                    stop=True,
-                )
+        zw, zs = {}, {}
 
-        def hand_out(c):
-            results[c] = res[c // 2][:, :, (c % 2) * P : (c % 2 + 1) * P]
-            (nc.vector.tensor_copy if c == 1 else nc.scalar.copy)(out=results[c], in_=acc[c][:])
-            if c % 2 == 1:
-                nc.sync.dma_start(out=out_rows[:, :, (c - 1) * P : (c + 1) * P], in_=res[c // 2][:])
+        def quantise_z(c):
+            zw[c] = keep.tile([P, P], U32, name="zw%d" % c, align_bytes=64)
+            zs[c] = keep.tile([P, P], U8, name="zs%d" % c, align_bytes=64)
+            nc.vector.quantize_mx(out=zw[c][:].bitcast(FP8X4), scales=zs[c][:], in_=z[c][:])
+
+        def second_product(into, c, t):
+            nc.tensor.matmul_mx(
+                out=into,
+                lhsT=w2w[:, 2 * P * t : 2 * P * (t + 1)].bitcast(FP4X4),
+                lhsT_scale=w2s[:, P * t : P * (t + 1)],
+                rhs=zw[c][:].bitcast(FP8X4),
+                rhs_scale=zs[c][:],
+                start=True,
+                stop=True,
+            )
+
+        def first_pair():
+            for half, engine_copy in enumerate((nc.scalar.copy, nc.vector.tensor_copy)):
+                ts = slice(2 * half, 2 * half + 2)
+                acc = psum.tile([P, 2, 2 * P], F32, name="acc", tag="bank%d" % (2 * half + 1))
+                for c in range(2):
+                    for t in range(2):
+                        second_product(acc[:, t, c * P : (c + 1) * P], c, 2 * half + t)
+                engine_copy(out=res[0][:, ts], in_=acc[:])
+                nc.sync.dma_start(out=out_rows[:, ts, 0 : 2 * P], in_=res[0][:, ts])
+
+        def second_pair():
+            for c in range(2):
+                acc = psum.tile([P, PACK, P], F32, name="acc", tag="bank%d" % (2 * c + 5))
+                for t in range(PACK):
+                    second_product(acc[:, t, :], 2 + c, t)
+                nc.scalar.copy(out=res[1][:, :, c * P : (c + 1) * P], in_=acc[:])
+            nc.sync.dma_start(out=out_rows[:, :, 2 * P :], in_=res[1][:])
 
         rounded = keep.tile([P, CHUNKS * PACK * P], BF16, name="rounded", align_bytes=64)
 
         def round_result(c):
             nc.vector.tensor_copy(
                 out=rounded[:, c * K_PASS : (c + 1) * K_PASS].rearrange("p (c i t) -> p c t i", i=4, t=PACK),
-                in_=results[c].rearrange("p t (c i) -> p c t i", i=4),
+                in_=res[c // 2][:, :, (c % 2) * P : (c % 2 + 1) * P].rearrange("p t (c i) -> p c t i", i=4),
             )
 
         def quantise_result(first, end):
@@ -236,10 +257,6 @@ def tile_picked_zbloom_none_po_kernel(
                 in_=rounded[:, first * K_PASS : end * K_PASS],
             )
 
-        def store_words(first, end):
-            feats = slice(first * P, end * P)
-            nc.sync.dma_start(out=out_words[:, feats], in_=ow[:, feats].bitcast(I32))
-
         for c in range(CHUNKS):
             finish_first(c)
         w2s = keep.tile([P, N], U8, name="w2s", tag="grouped11", align_bytes=64)
@@ -248,15 +265,19 @@ def tile_picked_zbloom_none_po_kernel(
             in_=w2s_raw[:].rearrange("p (m t) -> p t m", t=PACK),
         )
 
-        for stage in (turn, second_product, hand_out):
+        for stage in (turn, quantise_z):
             for c in range(CHUNKS):
                 stage(c)
-        for c in range(CHUNKS):
+        first_pair()
+        second_pair()
+        for c in range(3):
             round_result(c)
         quantise_result(0, 2)
+        nc.sync.dma_start(out=out_words[:, 0 : 2 * P], in_=ow[:, 0 : 2 * P].bitcast(I32))
+        round_result(3)
         quantise_result(2, 3)
         quantise_result(3, 4)
-        store_words(0, 4)
+        nc.sync.dma_start(out=out_words[:, 2 * P :], in_=ow[:, 2 * P :].bitcast(I32))
         for q in range(QUADS):
             nc.scalar.dma_start(
                 out=out_2[0, 4 * q : 4 * q + 4, :].bitcast(I32), in_=out_scales[32 * q : 32 * q + 4, :].bitcast(I32)

@@ -52,7 +52,7 @@ def tile_picked_zbloom_none_po_kernel(
             queue.dma_start(out=xs_table[g:32:PASSES, :].bitcast(I32), in_=x_scales[g].bitcast(I32))
         gate_rows = keep.tile([P, P], F32, name="gate_rows", align_bytes=64)
         nc.gpsimd.memset(gate_rows[:], 0.0)
-        nc.sync.dma_start(
+        nc.scalar.dma_start(
             out=gate_rows[0 : D * CHUNKS, :], in_=gate[:, 0, :].rearrange("d (c p) -> d c p", p=P)
         )
         ident = keep.tile([P, P], F32, name="ident")
@@ -243,8 +243,8 @@ def tile_picked_zbloom_none_po_kernel(
 
         rounded = keep.tile([P, CHUNKS * PACK * P], BF16, name="rounded", align_bytes=64)
 
-        def round_result(c):
-            nc.vector.tensor_copy(
+        def round_result(c, engine_copy):
+            engine_copy(
                 out=rounded[:, c * K_PASS : (c + 1) * K_PASS].rearrange("p (c i t) -> p c t i", i=4, t=PACK),
                 in_=res[c // 2][:, :, (c % 2) * P : (c % 2 + 1) * P].rearrange("p t (c i) -> p c t i", i=4),
             )
@@ -271,10 +271,10 @@ def tile_picked_zbloom_none_po_kernel(
         first_pair()
         second_pair()
         for c in range(3):
-            round_result(c)
+            round_result(c, nc.vector.tensor_copy)
         quantise_result(0, 2)
         nc.sync.dma_start(out=out_words[:, 0 : 2 * P], in_=ow[:, 0 : 2 * P].bitcast(I32))
-        round_result(3)
+        round_result(3, nc.scalar.copy)
         quantise_result(2, 3)
         quantise_result(3, 4)
         nc.sync.dma_start(out=out_words[:, 2 * P :], in_=ow[:, 2 * P :].bitcast(I32))

@@ -64,9 +64,9 @@ def tile_picked_zbloom_none_po_kernel(
         nc.scalar.dma_start(out=w2w_raw[:].bitcast(I32), in_=w2_words[0].bitcast(I32))
 
         w2w = keep.tile([P, 2 * N], U8, name="w2w", align_bytes=64)
-        nc.gpsimd.tensor_copy(
-            out=w2w[:].rearrange("p (t m b) -> p t m b", t=PACK, b=2),
-            in_=w2w_raw[:].rearrange("p (m t b) -> p t m b", t=PACK, b=2),
+        nc.scalar.copy(
+            out=w2w[:].bitcast(U16).rearrange("p (t m) -> p t m", t=PACK),
+            in_=w2w_raw[:].bitcast(U16).rearrange("p (m t) -> p t m", t=PACK),
         )
 
         xw_table = [keep.tile([P, T], I32, name="xw_table%d" % g, align_bytes=64) for g in range(PASSES)]
@@ -152,7 +152,7 @@ def tile_picked_zbloom_none_po_kernel(
             )
 
         unread = psum.tile([P, H], F32, name="unread", tag="bank7")
-        for n in range(4):
+        for n in range(2):
             nc.tensor.matmul_mx(
                 out=unread[:],
                 lhsT=xw[0][:, 0:P].bitcast(FP8X4),

@@ -25,6 +25,10 @@ PASSES = K // K_PASS
 CHUNKS = V // P
 QUADS = 4
 HALF = H // 2
+Y_BANK = ((0, 1, 2, 3), (4, 5, 0))
+LAST_BANKS = (2, 3)
+TURN_BANK = (6, 7, 1, 4)
+RESULT_BANK = (5, 0, 2, 3)
 
 
 def round_and_interleave(engine_copies, grouped, raw):
@@ -48,8 +52,8 @@ def tile_picked_zbloom_none_po_kernel(
         nc.sync.dma_start(offsets[:], offs)
 
         xs_table = keep.tile([P, T], U8, name="xs_table", align_bytes=64)
-        for g, queue in enumerate((nc.sync, nc.sync)):
-            queue.dma_start(out=xs_table[g:32:PASSES, :].bitcast(I32), in_=x_scales[g].bitcast(I32))
+        for g in range(PASSES):
+            nc.sync.dma_start(out=xs_table[g:32:PASSES, :].bitcast(I32), in_=x_scales[g].bitcast(I32))
         gate_rows = keep.tile([P, P], F32, name="gate_rows", align_bytes=64)
         nc.gpsimd.memset(gate_rows[:], 0.0)
         nc.scalar.dma_start(
@@ -59,10 +63,11 @@ def tile_picked_zbloom_none_po_kernel(
         make_identity(nc, ident[:])
         nc.vector.memset(xs_table[32:64, :].bitcast(I32), 0)
         nc.vector.memset(xs_table[64:128, :].bitcast(I32), 0)
+        xs = keep.tile([P, PASSES * S], U8, name="xs", align_bytes=64)
+        nc.gpsimd.memset(xs[:].bitcast(I32), 0)
 
         w2w_raw = keep.tile([P, 2 * N], U8, name="w2w_raw", align_bytes=64)
         nc.scalar.dma_start(out=w2w_raw[:].bitcast(I32), in_=w2_words[0].bitcast(I32))
-
         w2w = keep.tile([P, 2 * N], U8, name="w2w", align_bytes=64)
         nc.scalar.copy(
             out=w2w[:].bitcast(U16).rearrange("p (t m) -> p t m", t=PACK),
@@ -84,8 +89,6 @@ def tile_picked_zbloom_none_po_kernel(
         nc.tensor.transpose(gate_ps[:], gate_rows[:], ident[:])
         gate_cols = keep.tile([P, D * CHUNKS], F32, name="gate_cols")
         nc.scalar.activation(out=gate_cols[:], in_=gate_ps[:, 0 : D * CHUNKS], func=COPY)
-        xs = keep.tile([P, PASSES * S], U8, name="xs", tag="gate_rows", align_bytes=64)
-        nc.gpsimd.memset(xs[:].bitcast(I32), 0)
 
         load_x(0)
         raw00 = load_w1(0, 0, "stage0")
@@ -94,7 +97,7 @@ def tile_picked_zbloom_none_po_kernel(
         xs_picked = keep.tile([P, S], U8, name="xs_picked", align_bytes=64)
         nc.vector.tensor_copy(out=xs_picked[:], in_=xs_table[:].indirect(offsets[:]))
         for q in range(QUADS):
-            nc.scalar.dma_start(
+            nc.sync.dma_start(
                 out=xs[32 * q : 32 * q + 4, :].bitcast(I32),
                 in_=xs_picked[8 * q : 8 * q + 8, :].bitcast(I32),
             )
@@ -126,46 +129,51 @@ def tile_picked_zbloom_none_po_kernel(
         y = {}
         zt = [keep.tile([P, H], BF16, name="zt%d" % c) for c in range(CHUNKS)]
 
-        def first_product(c, d, g, h):
+        def first_pass(c, h, d, g, start, stop):
             cols = slice(d * V + c * P, d * V + (c + 1) * P)
             nc.tensor.matmul_mx(
-                out=y[c, d][:, h * HALF : (h + 1) * HALF],
+                out=y[c, h, d],
                 lhsT=xw[g][:, cols].bitcast(FP8X4),
                 lhsT_scale=xs[:, g * S + d * V + c * P : g * S + d * V + (c + 1) * P],
                 rhs=w1w[g, h][:].bitcast(FP8X4),
                 rhs_scale=w1s[g, h][:],
-                start=(g == 0),
-                stop=(g == PASSES - 1),
+                start=start,
+                stop=stop,
             )
 
-        def weigh(c, h):
-            half = slice(h * HALF, (h + 1) * HALF)
-            gated0 = keep.tile([P, HALF], F32, name="gated%d%d" % (c, h), align_bytes=64)
-            nc.scalar.activation(out=gated0[:], in_=y[c, 0][:, half], func=COPY, scale=gate_cols[:, c : c + 1])
+        def first_product(c, h, g):
+            if g == 0:
+                bank = psum.tile([P, D, HALF], F32, name="y", tag="bank%d" % Y_BANK[h][c])
+                for d in range(D):
+                    y[c, h, d] = bank[:, d, :]
+            for d in range(D):
+                first_pass(c, h, d, g, g == 0 and d == 0, g == PASSES - 1 and d == D - 1)
+
+        def last_product(c, h):
+            for d in range(D):
+                bank = psum.tile([P, HALF], F32, name="y_last", tag="bank%d" % LAST_BANKS[d])
+                y[c, h, d] = bank[:]
+                for g in range(PASSES):
+                    first_pass(c, h, d, g, g == 0, g == PASSES - 1)
+
+        gated = {}
+
+        def gate_first(c, h):
+            gated[c, h] = keep.tile([P, HALF], F32, name="gated%d%d" % (c, h), align_bytes=64)
+            nc.scalar.activation(out=gated[c, h][:], in_=y[c, h, 0], func=COPY, scale=gate_cols[:, c : c + 1])
+
+        def weighted_sum(c, h):
             nc.vector.scalar_tensor_tensor(
                 out=zt[c][:].rearrange("p (u h x) -> p h u x", u=2, h=2)[:, h],
-                in0=y[c, 1][:, half].rearrange("p (u x) -> p u x", u=2),
+                in0=y[c, h, 1].rearrange("p (u x) -> p u x", u=2),
                 scalar=gate_cols[:, CHUNKS + c : CHUNKS + c + 1],
-                in1=gated0[:].rearrange("p (u x) -> p u x", u=2),
+                in1=gated[c, h][:].rearrange("p (u x) -> p u x", u=2),
                 op0=MULT,
                 op1=ADD,
             )
 
-        unread = psum.tile([P, H], F32, name="unread", tag="bank7")
-        for n in range(2):
-            nc.tensor.matmul_mx(
-                out=unread[:],
-                lhsT=xw[0][:, 0:P].bitcast(FP8X4),
-                lhsT_scale=xs_picked[:, 0:P],
-                rhs=xw[0][:, 0:H].bitcast(FP8X4),
-                rhs_scale=xs_picked[:, 0:H],
-                start=True,
-                stop=True,
-            )
         for c in range(CHUNKS):
-            for d in range(D):
-                y[c, d] = psum.tile([P, H], F32, name="y", tag="bank%d" % (D * c + d))
-                first_product(c, d, 0, 0)
+            first_product(c, 0, 0)
         quantise_w1(1, 0, raw10, [nc.scalar.copy])
         w2s_raw = keep.tile([P, N], U8, name="w2s_raw", tag="xs_table", align_bytes=64)
         nc.gpsimd.memset(w2s_raw[:].bitcast(I32), 0)
@@ -174,13 +182,23 @@ def tile_picked_zbloom_none_po_kernel(
                 out=w2s_raw[32 * q : 32 * q + 4, :].bitcast(I32),
                 in_=w2_scales[0, 4 * q : 4 * q + 4, :].bitcast(I32),
             )
-
+        for c in range(CHUNKS):
+            first_product(c, 0, 1)
         quantise_w1(0, 1, raw01, [nc.scalar.copy])
         quantise_w1(1, 1, raw11, [nc.vector.tensor_copy])
         for c in range(CHUNKS):
-            for d in range(D):
-                first_product(c, d, 1, 0)
-            weigh(c, 0)
+            gate_first(c, 0)
+        for g in range(PASSES):
+            for c in range(2):
+                first_product(c, 1, g)
+        for c in range(CHUNKS):
+            weighted_sum(c, 0)
+        for g in range(PASSES):
+            first_product(2, 1, g)
+        last_product(3, 1)
+        for c in range(CHUNKS):
+            gate_first(c, 1)
+            weighted_sum(c, 1)
 
         out_rows = out_0.rearrange("(p t) v -> p t v", t=PACK)
         out_words = out_1[0].rearrange("p n t -> p (n t)").bitcast(I32)
@@ -188,16 +206,10 @@ def tile_picked_zbloom_none_po_kernel(
         ow = keep.tile([P, V], U32, name="ow", align_bytes=64)
         res = [keep.tile([P, PACK, 2 * P], F32, name="res%d" % n) for n in range(2)]
 
-        def finish_first(c):
-            for d in range(D):
-                for g in range(PASSES):
-                    first_product(c, d, g, 1)
-            weigh(c, 1)
-
         z = [keep.tile([P, PACK * P], BF16, name="z%d" % c, align_bytes=64) for c in range(CHUNKS)]
 
         def turn(c):
-            turned = psum.tile([P, 2, P], F32, name="turned", tag="bank%d" % (D * c))
+            turned = psum.tile([P, 2, P], F32, name="turned", tag="bank%d" % TURN_BANK[c])
             for u in range(2):
                 nc.tensor.transpose(turned[:, u, :], zt[c][:].bitcast(F32)[:, u * P : (u + 1) * P], ident[:])
             nc.scalar.copy(
@@ -226,7 +238,7 @@ def tile_picked_zbloom_none_po_kernel(
         def first_pair():
             for half, engine_copy in enumerate((nc.scalar.copy, nc.vector.tensor_copy)):
                 ts = slice(2 * half, 2 * half + 2)
-                acc = psum.tile([P, 2, 2 * P], F32, name="acc", tag="bank%d" % (2 * half + 1))
+                acc = psum.tile([P, 2, 2 * P], F32, name="acc", tag="bank%d" % RESULT_BANK[half])
                 for c in range(2):
                     for t in range(2):
                         second_product(acc[:, t, c * P : (c + 1) * P], c, 2 * half + t)
@@ -235,7 +247,7 @@ def tile_picked_zbloom_none_po_kernel(
 
         def second_pair():
             for c in range(2):
-                acc = psum.tile([P, PACK, P], F32, name="acc", tag="bank%d" % (2 * c + 5))
+                acc = psum.tile([P, PACK, P], F32, name="acc", tag="bank%d" % RESULT_BANK[2 + c])
                 for t in range(PACK):
                     second_product(acc[:, t, :], 2 + c, t)
                 nc.scalar.copy(out=res[1][:, :, c * P : (c + 1) * P], in_=acc[:])
@@ -257,8 +269,6 @@ def tile_picked_zbloom_none_po_kernel(
                 in_=rounded[:, first * K_PASS : end * K_PASS],
             )
 
-        for c in range(CHUNKS):
-            finish_first(c)
         w2s = keep.tile([P, N], U8, name="w2s", tag="grouped11", align_bytes=64)
         nc.gpsimd.tensor_copy(
             out=w2s[:].rearrange("p (t m) -> p t m", t=PACK),

@@ -25,6 +25,7 @@ PASSES = K // K_PASS
 CHUNKS = V // P
 QUADS = 4
 HALF = H // 2
+ALIGN = 256
 Y_BANK = ((0, 1, 2, 3), (4, 5, 0))
 LAST_BANKS = (2, 3)
 TURN_BANK = (6, 7, 1, 4)
@@ -48,53 +49,53 @@ def tile_picked_zbloom_none_po_kernel(
         keep = ctx.enter_context(tc.tile_pool(name="keep", bufs=1))
         psum = ctx.enter_context(tc.psum_pool(name="psum", bufs=1))
 
-        offsets = keep.tile([P, S // 16], U16, name="offsets")
+        offsets = keep.tile([P, S // 16], U16, name="offsets", align_bytes=ALIGN)
         nc.sync.dma_start(offsets[:], offs)
 
-        xs_table = keep.tile([P, T], U8, name="xs_table", align_bytes=64)
+        xs_table = keep.tile([P, T], U8, name="xs_table", align_bytes=ALIGN)
         for g in range(PASSES):
             nc.sync.dma_start(out=xs_table[g:32:PASSES, :].bitcast(I32), in_=x_scales[g].bitcast(I32))
-        gate_rows = keep.tile([P, P], F32, name="gate_rows", align_bytes=64)
+        gate_rows = keep.tile([P, P], F32, name="gate_rows", align_bytes=ALIGN)
         nc.gpsimd.memset(gate_rows[:], 0.0)
         nc.scalar.dma_start(
             out=gate_rows[0 : D * CHUNKS, :], in_=gate[:, 0, :].rearrange("d (c p) -> d c p", p=P)
         )
-        ident = keep.tile([P, P], F32, name="ident")
+        ident = keep.tile([P, P], F32, name="ident", align_bytes=ALIGN)
         make_identity(nc, ident[:])
         nc.vector.memset(xs_table[32:64, :].bitcast(I32), 0)
         nc.vector.memset(xs_table[64:128, :].bitcast(I32), 0)
-        xs = keep.tile([P, PASSES * S], U8, name="xs", align_bytes=64)
+        xs = keep.tile([P, PASSES * S], U8, name="xs", align_bytes=ALIGN)
         nc.gpsimd.memset(xs[:].bitcast(I32), 0)
 
-        w2w_raw = keep.tile([P, 2 * N], U8, name="w2w_raw", align_bytes=64)
+        w2w_raw = keep.tile([P, 2 * N], U8, name="w2w_raw", align_bytes=ALIGN)
         nc.scalar.dma_start(out=w2w_raw[:].bitcast(I32), in_=w2_words[0].bitcast(I32))
-        w2w = keep.tile([P, 2 * N], U8, name="w2w", align_bytes=64)
+        w2w = keep.tile([P, 2 * N], U8, name="w2w", align_bytes=ALIGN)
         nc.scalar.copy(
             out=w2w[:].bitcast(U16).rearrange("p (t m) -> p t m", t=PACK),
             in_=w2w_raw[:].bitcast(U16).rearrange("p (m t) -> p t m", t=PACK),
         )
 
-        xw_table = [keep.tile([P, T], I32, name="xw_table%d" % g, align_bytes=64) for g in range(PASSES)]
+        xw_table = [keep.tile([P, T], I32, name="xw_table%d" % g, align_bytes=ALIGN) for g in range(PASSES)]
         w1_rows = [w1[g * K_PASS : (g + 1) * K_PASS, :].rearrange("(p j) c -> p j c", j=PACK) for g in range(PASSES)]
 
         def load_x(g):
             nc.sync.dma_start(out=xw_table[g][:], in_=x_words[g].rearrange("p n t -> p (n t)").bitcast(I32))
 
         def load_w1(g, h, tag):
-            raw = keep.tile([P, PACK, HALF], F32, name="w1_raw%d%d" % (g, h), tag=tag, align_bytes=64)
+            raw = keep.tile([P, PACK, HALF], F32, name="w1_raw%d%d" % (g, h), tag=tag, align_bytes=ALIGN)
             nc.sync.dma_start(out=raw[:], in_=w1_rows[g][:, :, h * HALF : (h + 1) * HALF])
             return raw[:]
 
         gate_ps = psum.tile([P, P], F32, name="gate_ps", tag="bank7")
         nc.tensor.transpose(gate_ps[:], gate_rows[:], ident[:])
-        gate_cols = keep.tile([P, D * CHUNKS], F32, name="gate_cols")
+        gate_cols = keep.tile([P, D * CHUNKS], F32, name="gate_cols", align_bytes=ALIGN)
         nc.scalar.activation(out=gate_cols[:], in_=gate_ps[:, 0 : D * CHUNKS], func=COPY)
 
         load_x(0)
         raw00 = load_w1(0, 0, "stage0")
         load_x(1)
 
-        xs_picked = keep.tile([P, S], U8, name="xs_picked", align_bytes=64)
+        xs_picked = keep.tile([P, S], U8, name="xs_picked", align_bytes=ALIGN)
         nc.vector.tensor_copy(out=xs_picked[:], in_=xs_table[:].indirect(offsets[:]))
         for q in range(QUADS):
             nc.sync.dma_start(
@@ -103,7 +104,7 @@ def tile_picked_zbloom_none_po_kernel(
             )
 
         def gather_words(g, tag):
-            picked = keep.tile([P, S], U32, name="xw%d" % g, tag=tag, align_bytes=64)
+            picked = keep.tile([P, S], U32, name="xw%d" % g, tag=tag, align_bytes=ALIGN)
             nc.vector.tensor_copy(out=picked[:], in_=xw_table[g][:].bitcast(U32).indirect(offsets[:]))
             return picked
 
@@ -113,21 +114,21 @@ def tile_picked_zbloom_none_po_kernel(
         w1w, w1s = {}, {}
 
         def quantise_w1(g, h, raw, engine_copy):
-            grouped = keep.tile([P, PACK * HALF], BF16, name="grouped%d%d" % (g, h), align_bytes=64)
+            grouped = keep.tile([P, PACK * HALF], BF16, name="grouped%d%d" % (g, h), align_bytes=ALIGN)
             round_and_interleave(engine_copy, grouped[:], raw)
-            w1w[g, h] = keep.tile([P, HALF], U32, name="w1w%d%d" % (g, h), align_bytes=64)
-            w1s[g, h] = keep.tile([P, HALF], U8, name="w1s%d%d" % (g, h), align_bytes=64)
+            w1w[g, h] = keep.tile([P, HALF], U32, name="w1w%d%d" % (g, h), align_bytes=ALIGN)
+            w1s[g, h] = keep.tile([P, HALF], U8, name="w1s%d%d" % (g, h), align_bytes=ALIGN)
             nc.vector.quantize_mx(out=w1w[g, h][:].bitcast(FP8X4), scales=w1s[g, h][:], in_=grouped[:])
 
         quantise_w1(0, 0, raw00, [nc.scalar.copy])
-        late = keep.tile([P, PASSES, PACK, HALF], F32, name="late", tag="stage0", align_bytes=64)
+        late = keep.tile([P, PASSES, PACK, HALF], F32, name="late", tag="stage0", align_bytes=ALIGN)
         for g in range(PASSES):
             nc.sync.dma_start(out=late[:, g], in_=w1_rows[g][:, :, HALF:])
         raw01, raw11 = late[:, 0], late[:, 1]
         xw.append(gather_words(1, "grouped00"))
 
         y = {}
-        zt = [keep.tile([P, H], BF16, name="zt%d" % c) for c in range(CHUNKS)]
+        zt = [keep.tile([P, H], BF16, name="zt%d" % c, align_bytes=ALIGN) for c in range(CHUNKS)]
 
         def first_pass(c, h, d, g, start, stop):
             cols = slice(d * V + c * P, d * V + (c + 1) * P)
@@ -159,7 +160,7 @@ def tile_picked_zbloom_none_po_kernel(
         gated = {}
 
         def gate_first(c, h):
-            gated[c, h] = keep.tile([P, HALF], F32, name="gated%d%d" % (c, h), align_bytes=64)
+            gated[c, h] = keep.tile([P, HALF], F32, name="gated%d%d" % (c, h), align_bytes=ALIGN)
             nc.scalar.activation(out=gated[c, h][:], in_=y[c, h, 0], func=COPY, scale=gate_cols[:, c : c + 1])
 
         def weighted_sum(c, h):
@@ -175,7 +176,7 @@ def tile_picked_zbloom_none_po_kernel(
         for c in range(CHUNKS):
             first_product(c, 0, 0)
         quantise_w1(1, 0, raw10, [nc.scalar.copy])
-        w2s_raw = keep.tile([P, N], U8, name="w2s_raw", tag="xs_table", align_bytes=64)
+        w2s_raw = keep.tile([P, N], U8, name="w2s_raw", tag="xs_table", align_bytes=ALIGN)
         nc.gpsimd.memset(w2s_raw[:].bitcast(I32), 0)
         for q in range(QUADS):
             nc.sync.dma_start(
@@ -202,11 +203,11 @@ def tile_picked_zbloom_none_po_kernel(
 
         out_rows = out_0.rearrange("(p t) v -> p t v", t=PACK)
         out_words = out_1[0].rearrange("p n t -> p (n t)").bitcast(I32)
-        out_scales = keep.tile([P, V], U8, name="out_scales", align_bytes=64)
-        ow = keep.tile([P, V], U32, name="ow", align_bytes=64)
-        res = [keep.tile([P, PACK, 2 * P], F32, name="res%d" % n) for n in range(2)]
+        out_scales = keep.tile([P, V], U8, name="out_scales", align_bytes=ALIGN)
+        ow = keep.tile([P, V], U32, name="ow", align_bytes=ALIGN)
+        res = [keep.tile([P, PACK, 2 * P], F32, name="res%d" % n, align_bytes=ALIGN) for n in range(2)]
 
-        z = [keep.tile([P, PACK * P], BF16, name="z%d" % c, align_bytes=64) for c in range(CHUNKS)]
+        z = [keep.tile([P, PACK * P], BF16, name="z%d" % c, align_bytes=ALIGN) for c in range(CHUNKS)]
 
         def turn(c):
             turned = psum.tile([P, 2, P], F32, name="turned", tag="bank%d" % TURN_BANK[c])
@@ -220,8 +221,8 @@ def tile_picked_zbloom_none_po_kernel(
         zw, zs = {}, {}
 
         def quantise_z(c):
-            zw[c] = keep.tile([P, P], U32, name="zw%d" % c, align_bytes=64)
-            zs[c] = keep.tile([P, P], U8, name="zs%d" % c, align_bytes=64)
+            zw[c] = keep.tile([P, P], U32, name="zw%d" % c, align_bytes=ALIGN)
+            zs[c] = keep.tile([P, P], U8, name="zs%d" % c, align_bytes=ALIGN)
             nc.vector.quantize_mx(out=zw[c][:].bitcast(FP8X4), scales=zs[c][:], in_=z[c][:])
 
         def second_product(into, c, t):
@@ -253,7 +254,7 @@ def tile_picked_zbloom_none_po_kernel(
                 nc.scalar.copy(out=res[1][:, :, c * P : (c + 1) * P], in_=acc[:])
             nc.sync.dma_start(out=out_rows[:, :, 2 * P :], in_=res[1][:])
 
-        rounded = keep.tile([P, CHUNKS * PACK * P], BF16, name="rounded", align_bytes=64)
+        rounded = keep.tile([P, CHUNKS * PACK * P], BF16, name="rounded", align_bytes=ALIGN)
 
         def round_result(c, engine_copy):
             engine_copy(
@@ -269,7 +270,7 @@ def tile_picked_zbloom_none_po_kernel(
                 in_=rounded[:, first * K_PASS : end * K_PASS],
             )
 
-        w2s = keep.tile([P, N], U8, name="w2s", tag="grouped11", align_bytes=64)
+        w2s = keep.tile([P, N], U8, name="w2s", tag="grouped11", align_bytes=ALIGN)
         nc.gpsimd.tensor_copy(
             out=w2s[:].rearrange("p (t m) -> p t m", t=PACK),
             in_=w2s_raw[:].rearrange("p (m t) -> p t m", t=PACK),

@@ -237,21 +237,25 @@ def tile_picked_zbloom_none_po_kernel(
             )
 
         def first_pair():
-            for half, engine_copy in enumerate((nc.scalar.copy, nc.vector.tensor_copy)):
-                ts = slice(2 * half, 2 * half + 2)
-                acc = psum.tile([P, 2, 2 * P], F32, name="acc", tag="bank%d" % RESULT_BANK[half])
+            for bank, slots, engine_copy in (
+                (TURN_BANK[0], range(0, 1), nc.scalar.copy),
+                (RESULT_BANK[0], range(1, 2), nc.scalar.copy),
+                (RESULT_BANK[1], range(2, PACK), nc.vector.tensor_copy),
+            ):
+                acc = psum.tile([P, len(slots), 2 * P], F32, name="acc", tag="bank%d" % bank)
                 for c in range(2):
-                    for t in range(2):
-                        second_product(acc[:, t, c * P : (c + 1) * P], c, 2 * half + t)
+                    for n, t in enumerate(slots):
+                        second_product(acc[:, n, c * P : (c + 1) * P], c, t)
+                ts = slice(slots.start, slots.stop)
                 engine_copy(out=res[0][:, ts], in_=acc[:])
                 nc.sync.dma_start(out=out_rows[:, ts, 0 : 2 * P], in_=res[0][:, ts])
 
         def second_pair():
-            for c in range(2):
+            for c, engine_copy in enumerate((nc.scalar.copy, nc.vector.tensor_copy)):
                 acc = psum.tile([P, PACK, P], F32, name="acc", tag="bank%d" % RESULT_BANK[2 + c])
                 for t in range(PACK):
                     second_product(acc[:, t, :], 2 + c, t)
-                nc.scalar.copy(out=res[1][:, :, c * P : (c + 1) * P], in_=acc[:])
+                engine_copy(out=res[1][:, :, c * P : (c + 1) * P], in_=acc[:])
             nc.sync.dma_start(out=out_rows[:, :, 2 * P :], in_=res[1][:])
 
         rounded = keep.tile([P, CHUNKS * PACK * P], BF16, name="rounded", align_bytes=ALIGN)
@@ -281,14 +285,12 @@ def tile_picked_zbloom_none_po_kernel(
                 stage(c)
         first_pair()
         second_pair()
-        for c in range(3):
-            round_result(c, nc.vector.tensor_copy)
+        for c in range(CHUNKS):
+            round_result(c, nc.vector.tensor_copy if c % 2 else nc.scalar.copy)
         quantise_result(0, 2)
-        nc.sync.dma_start(out=out_words[:, 0 : 2 * P], in_=ow[:, 0 : 2 * P].bitcast(I32))
-        round_result(3, nc.scalar.copy)
-        quantise_result(2, 3)
         quantise_result(3, 4)
-        nc.sync.dma_start(out=out_words[:, 2 * P :], in_=ow[:, 2 * P :].bitcast(I32))
+        quantise_result(2, 3)
+        nc.sync.dma_start(out=out_words, in_=ow[:].bitcast(I32))
         for q in range(QUADS):
             nc.scalar.dma_start(
                 out=out_2[0, 4 * q : 4 * q + 4, :].bitcast(I32), in_=out_scales[32 * q : 32 * q + 4, :].bitcast(I32)

from contextlib import ExitStack

import concourse.mybir as mybir
from concourse.masks import make_identity

K, T, S, D, V, H, N = 1024, 2048, 1024, 2, 512, 512, 512
FLOPS = 2 * K * H * S + 2 * H * N * V

F32 = mybir.dt.float32
BF16 = mybir.dt.bfloat16
I32 = mybir.dt.int32
U32 = mybir.dt.uint32
U16 = mybir.dt.uint16
U8 = mybir.dt.uint8
FP8X4 = mybir.dt.float8_e4m3fn_x4
FP4X4 = mybir.dt.float4_e2m1fn_x4
COPY = mybir.ActivationFunctionType.Copy
MULT = mybir.AluOpType.mult
ADD = mybir.AluOpType.add

P = 128
PACK = 4
K_PASS = P * PACK
PASSES = K // K_PASS
CHUNKS = V // P
QUADS = 4
HALF = H // 2
ALIGN = 256
Y_BANK = ((0, 1, 2, 3), (4, 5, 0))
LAST_BANKS = (2, 3)
TURN_BANK = (6, 7, 1, 4)
RESULT_BANK = (5, 0, 2, 3)


def round_and_interleave(engine_copies, grouped, raw):
    dst = grouped.rearrange("p (u m e j) -> p m j u e", u=2, e=2, j=PACK)
    src = raw.rearrange("p j (m u e) -> p m j u e", u=2, e=2)
    share = 2 // len(engine_copies)
    for n, engine_copy in enumerate(engine_copies):
        us = slice(n * share, (n + 1) * share)
        engine_copy(out=dst[:, :, :, us, :], in_=src[:, :, :, us, :])


def tile_picked_zbloom_none_po_kernel(
    tc, x_words, x_scales, w1, w2_words, w2_scales, gate, offs, out_0, out_1, out_2
):
    nc = tc.nc
    with ExitStack() as ctx:
        keep = ctx.enter_context(tc.tile_pool(name="keep", bufs=1))
        psum = ctx.enter_context(tc.psum_pool(name="psum", bufs=1))

        offsets = keep.tile([P, S // 16], U16, name="offsets", align_bytes=ALIGN)
        nc.sync.dma_start(offsets[:], offs)

        xs_table = keep.tile([P, T], U8, name="xs_table", align_bytes=ALIGN)
        for g in range(PASSES):
            nc.sync.dma_start(out=xs_table[g:32:PASSES, :].bitcast(I32), in_=x_scales[g].bitcast(I32))
        gate_rows = keep.tile([P, P], F32, name="gate_rows", align_bytes=ALIGN)
        nc.gpsimd.memset(gate_rows[:], 0.0)
        nc.scalar.dma_start(
            out=gate_rows[0 : D * CHUNKS, :], in_=gate[:, 0, :].rearrange("d (c p) -> d c p", p=P)
        )
        ident = keep.tile([P, P], F32, name="ident", align_bytes=ALIGN)
        make_identity(nc, ident[:])
        nc.vector.memset(xs_table[32:64, :].bitcast(I32), 0)
        nc.vector.memset(xs_table[64:128, :].bitcast(I32), 0)
        xs = keep.tile([P, PASSES * S], U8, name="xs", align_bytes=ALIGN)
        nc.gpsimd.memset(xs[:].bitcast(I32), 0)

        w2w_raw = keep.tile([P, 2 * N], U8, name="w2w_raw", align_bytes=ALIGN)
        nc.scalar.dma_start(out=w2w_raw[:].bitcast(I32), in_=w2_words[0].bitcast(I32))
        w2w = keep.tile([P, 2 * N], U8, name="w2w", align_bytes=ALIGN)
        nc.scalar.copy(
            out=w2w[:].bitcast(U16).rearrange("p (t m) -> p t m", t=PACK),
            in_=w2w_raw[:].bitcast(U16).rearrange("p (m t) -> p t m", t=PACK),
        )

        xw_table = [keep.tile([P, T], I32, name="xw_table%d" % g, align_bytes=ALIGN) for g in range(PASSES)]
        w1_rows = [w1[g * K_PASS : (g + 1) * K_PASS, :].rearrange("(p j) c -> p j c", j=PACK) for g in range(PASSES)]

        def load_x(g):
            nc.sync.dma_start(out=xw_table[g][:], in_=x_words[g].rearrange("p n t -> p (n t)").bitcast(I32))

        def load_w1(g, h, tag):
            raw = keep.tile([P, PACK, HALF], F32, name="w1_raw%d%d" % (g, h), tag=tag, align_bytes=ALIGN)
            nc.sync.dma_start(out=raw[:], in_=w1_rows[g][:, :, h * HALF : (h + 1) * HALF])
            return raw[:]

        gate_ps = psum.tile([P, P], F32, name="gate_ps", tag="bank7")
        nc.tensor.transpose(gate_ps[:], gate_rows[:], ident[:])
        gate_cols = keep.tile([P, D * CHUNKS], F32, name="gate_cols", align_bytes=ALIGN)
        nc.scalar.activation(out=gate_cols[:], in_=gate_ps[:, 0 : D * CHUNKS], func=COPY)

        load_x(0)
        raw00 = load_w1(0, 0, "stage0")
        load_x(1)

        xs_picked = keep.tile([P, S], U8, name="xs_picked", align_bytes=ALIGN)
        nc.vector.tensor_copy(out=xs_picked[:], in_=xs_table[:].indirect(offsets[:]))
        for q in range(QUADS):
            nc.sync.dma_start(
                out=xs[32 * q : 32 * q + 4, :].bitcast(I32),
                in_=xs_picked[8 * q : 8 * q + 8, :].bitcast(I32),
            )

        def gather_words(g, tag):
            picked = keep.tile([P, S], U32, name="xw%d" % g, tag=tag, align_bytes=ALIGN)
            nc.vector.tensor_copy(out=picked[:], in_=xw_table[g][:].bitcast(U32).indirect(offsets[:]))
            return picked

        xw = [gather_words(0, "xw0")]
        raw10 = load_w1(1, 0, "xs_table")

        w1w, w1s = {}, {}

        def quantise_w1(g, h, raw, engine_copy):
            grouped = keep.tile([P, PACK * HALF], BF16, name="grouped%d%d" % (g, h), align_bytes=ALIGN)
            round_and_interleave(engine_copy, grouped[:], raw)
            w1w[g, h] = keep.tile([P, HALF], U32, name="w1w%d%d" % (g, h), align_bytes=ALIGN)
            w1s[g, h] = keep.tile([P, HALF], U8, name="w1s%d%d" % (g, h), align_bytes=ALIGN)
            nc.vector.quantize_mx(out=w1w[g, h][:].bitcast(FP8X4), scales=w1s[g, h][:], in_=grouped[:])

        quantise_w1(0, 0, raw00, [nc.scalar.copy])
        late = keep.tile([P, PASSES, PACK, HALF], F32, name="late", tag="stage0", align_bytes=ALIGN)
        for g in range(PASSES):
            nc.sync.dma_start(out=late[:, g], in_=w1_rows[g][:, :, HALF:])
        raw01, raw11 = late[:, 0], late[:, 1]
        xw.append(gather_words(1, "grouped00"))

        y = {}
        zt = [keep.tile([P, H], BF16, name="zt%d" % c, align_bytes=ALIGN) for c in range(CHUNKS)]

        def first_pass(c, h, d, g, start, stop):
            cols = slice(d * V + c * P, d * V + (c + 1) * P)
            nc.tensor.matmul_mx(
                out=y[c, h, d],
                lhsT=xw[g][:, cols].bitcast(FP8X4),
                lhsT_scale=xs[:, g * S + d * V + c * P : g * S + d * V + (c + 1) * P],
                rhs=w1w[g, h][:].bitcast(FP8X4),
                rhs_scale=w1s[g, h][:],
                start=start,
                stop=stop,
            )

        def first_product(c, h, g):
            if g == 0:
                bank = psum.tile([P, D, HALF], F32, name="y", tag="bank%d" % Y_BANK[h][c])
                for d in range(D):
                    y[c, h, d] = bank[:, d, :]
            for d in range(D):
                first_pass(c, h, d, g, g == 0 and d == 0, g == PASSES - 1 and d == D - 1)

        def last_product(c, h):
            for d in range(D):
                bank = psum.tile([P, HALF], F32, name="y_last", tag="bank%d" % LAST_BANKS[d])
                y[c, h, d] = bank[:]
                for g in range(PASSES):
                    first_pass(c, h, d, g, g == 0, g == PASSES - 1)

        gated = {}

        def gate_first(c, h):
            gated[c, h] = keep.tile([P, HALF], F32, name="gated%d%d" % (c, h), align_bytes=ALIGN)
            nc.scalar.activation(out=gated[c, h][:], in_=y[c, h, 0], func=COPY, scale=gate_cols[:, c : c + 1])

        def weighted_sum(c, h):
            nc.vector.scalar_tensor_tensor(
                out=zt[c][:].rearrange("p (u h x) -> p h u x", u=2, h=2)[:, h],
                in0=y[c, h, 1].rearrange("p (u x) -> p u x", u=2),
                scalar=gate_cols[:, CHUNKS + c : CHUNKS + c + 1],
                in1=gated[c, h][:].rearrange("p (u x) -> p u x", u=2),
                op0=MULT,
                op1=ADD,
            )

        for c in range(CHUNKS):
            first_product(c, 0, 0)
        quantise_w1(1, 0, raw10, [nc.scalar.copy])
        w2s_raw = keep.tile([P, N], U8, name="w2s_raw", tag="xs_table", align_bytes=ALIGN)
        nc.gpsimd.memset(w2s_raw[:].bitcast(I32), 0)
        for q in range(QUADS):
            nc.sync.dma_start(
                out=w2s_raw[32 * q : 32 * q + 4, :].bitcast(I32),
                in_=w2_scales[0, 4 * q : 4 * q + 4, :].bitcast(I32),
            )
        for c in range(CHUNKS):
            first_product(c, 0, 1)
        quantise_w1(0, 1, raw01, [nc.scalar.copy])
        quantise_w1(1, 1, raw11, [nc.vector.tensor_copy])
        for c in range(CHUNKS):
            gate_first(c, 0)
        for g in range(PASSES):
            for c in range(2):
                first_product(c, 1, g)
        for c in range(CHUNKS):
            weighted_sum(c, 0)
        for g in range(PASSES):
            first_product(2, 1, g)
        last_product(3, 1)
        for c in range(CHUNKS):
            gate_first(c, 1)
            weighted_sum(c, 1)

        out_rows = out_0.rearrange("(p t) v -> p t v", t=PACK)
        out_words = out_1[0].rearrange("p n t -> p (n t)").bitcast(I32)
        out_scales = keep.tile([P, V], U8, name="out_scales", align_bytes=ALIGN)
        ow = keep.tile([P, V], U32, name="ow", align_bytes=ALIGN)
        res = [keep.tile([P, PACK, 2 * P], F32, name="res%d" % n, align_bytes=ALIGN) for n in range(2)]

        z = [keep.tile([P, PACK * P], BF16, name="z%d" % c, align_bytes=ALIGN) for c in range(CHUNKS)]

        def turn(c):
            turned = psum.tile([P, 2, P], F32, name="turned", tag="bank%d" % TURN_BANK[c])
            for u in range(2):
                nc.tensor.transpose(turned[:, u, :], zt[c][:].bitcast(F32)[:, u * P : (u + 1) * P], ident[:])
            nc.scalar.copy(
                out=z[c][:].bitcast(F32).rearrange("p (v u) -> p v u", u=2),
                in_=turned[:].rearrange("p u v -> p v u"),
            )

        zw, zs = {}, {}

        def quantise_z(c):
            zw[c] = keep.tile([P, P], U32, name="zw%d" % c, align_bytes=ALIGN)
            zs[c] = keep.tile([P, P], U8, name="zs%d" % c, align_bytes=ALIGN)
            nc.vector.quantize_mx(out=zw[c][:].bitcast(FP8X4), scales=zs[c][:], in_=z[c][:])

        def second_product(into, c, t):
            nc.tensor.matmul_mx(
                out=into,
                lhsT=w2w[:, 2 * P * t : 2 * P * (t + 1)].bitcast(FP4X4),
                lhsT_scale=w2s[:, P * t : P * (t + 1)],
                rhs=zw[c][:].bitcast(FP8X4),
                rhs_scale=zs[c][:],
                start=True,
                stop=True,
            )

        def first_pair():
            for bank, slots, engine_copy in (
                (TURN_BANK[0], range(0, 1), nc.scalar.copy),
                (RESULT_BANK[0], range(1, 2), nc.scalar.copy),
                (RESULT_BANK[1], range(2, PACK), nc.vector.tensor_copy),
            ):
                acc = psum.tile([P, len(slots), 2 * P], F32, name="acc", tag="bank%d" % bank)
                for c in range(2):
                    for n, t in enumerate(slots):
                        second_product(acc[:, n, c * P : (c + 1) * P], c, t)
                ts = slice(slots.start, slots.stop)
                engine_copy(out=res[0][:, ts], in_=acc[:])
                nc.sync.dma_start(out=out_rows[:, ts, 0 : 2 * P], in_=res[0][:, ts])

        def second_pair():
            for c, engine_copy in enumerate((nc.scalar.copy, nc.vector.tensor_copy)):
                acc = psum.tile([P, PACK, P], F32, name="acc", tag="bank%d" % RESULT_BANK[2 + c])
                for t in range(PACK):
                    second_product(acc[:, t, :], 2 + c, t)
                engine_copy(out=res[1][:, :, c * P : (c + 1) * P], in_=acc[:])
            nc.sync.dma_start(out=out_rows[:, :, 2 * P :], in_=res[1][:])

        rounded = keep.tile([P, CHUNKS * PACK * P], BF16, name="rounded", align_bytes=ALIGN)

        def round_result(c, engine_copy):
            engine_copy(
                out=rounded[:, c * K_PASS : (c + 1) * K_PASS].rearrange("p (c i t) -> p c t i", i=4, t=PACK),
                in_=res[c // 2][:, :, (c % 2) * P : (c % 2 + 1) * P].rearrange("p t (c i) -> p c t i", i=4),
            )

        def quantise_result(first, end):
            feats = slice(first * P, end * P)
            nc.vector.quantize_mx(
                out=ow[:, feats].bitcast(FP8X4),
                scales=out_scales[:, feats],
                in_=rounded[:, first * K_PASS : end * K_PASS],
            )

        w2s = keep.tile([P, N], U8, name="w2s", tag="grouped11", align_bytes=ALIGN)
        nc.gpsimd.tensor_copy(
            out=w2s[:].rearrange("p (t m) -> p t m", t=PACK),
            in_=w2s_raw[:].rearrange("p (m t) -> p t m", t=PACK),
        )

        for stage in (turn, quantise_z):
            for c in range(CHUNKS):
                stage(c)
        first_pair()
        second_pair()
        for c in range(CHUNKS):
            round_result(c, nc.vector.tensor_copy if c % 2 else nc.scalar.copy)
        quantise_result(0, 2)
        quantise_result(3, 4)
        quantise_result(2, 3)
        nc.sync.dma_start(out=out_words, in_=ow[:].bitcast(I32))
        for q in range(QUADS):
            nc.scalar.dma_start(
                out=out_2[0, 4 * q : 4 * q + 4, :].bitcast(I32), in_=out_scales[32 * q : 32 * q + 4, :].bitcast(I32)
            )
